import numpy as np
import ml_dtypes


def mxq(x, axis, fmt="e4m3"):
    dtype, down = {"e4m3": (ml_dtypes.float8_e4m3fn, 7), "e5m2": (ml_dtypes.float8_e5m2, 14)}[fmt]
    v = np.moveaxis(np.asarray(x, np.float32).astype(ml_dtypes.bfloat16).astype(np.float64), axis, -1)
    blocks = v.reshape(v.shape[:-1] + (-1, 32))
    amax = np.abs(blocks).max(-1, keepdims=True)
    byte = np.maximum(np.where(amax > 0, np.frexp(amax)[1] - 1 + 127, 0) - down, 1)
    scale = np.exp2(byte - 127.0)
    codes = (blocks / scale).astype(np.float32).astype(dtype).astype(np.float64)
    return np.moveaxis((codes * scale).reshape(v.shape), -1, axis)


WIDE = False


def mx_kscale(k):
    if not WIDE:
        return np.ones(k)
    levels = np.array([10, -10, 5, -5, 0])
    if k % 512:
        return np.exp2(np.random.permutation(np.resize(levels, k // 32))).repeat(32)
    a = np.empty((k // 512, 16))
    for p in range(k // 512):
        a[p, :8] = np.random.permutation(np.resize(levels, 8))
        for g in range(8):
            far = levels[np.abs(levels - a[p, g]) >= 10]
            a[p, g + 8] = far[np.random.randint(len(far))]
    return np.exp2(a.ravel()).repeat(32)


def f64(x):
    return np.asarray(x).astype(np.float64)


def striped(idx):
    return np.tile(idx.reshape(-1, 16).T, (8, 1)).astype(np.uint16)


def unstriped(offs):
    return offs[:16].T.reshape(-1).astype(np.int64)


def striped8(idx):
    return np.concatenate([x.reshape(-1, 16).T for x in idx]).astype(np.uint16)


def runs(offs, k):
    lists = np.stack([offs[16 * r : 16 * r + 16].T.reshape(-1) for r in range(8)]).astype(np.int64)
    return lists[np.arange(k) % 512 // 64]


def pack_weight(w):
    k, n = w.shape
    w = f64(np.asarray(w, np.float32).astype(ml_dtypes.bfloat16)).reshape(k // 32, 32, n)
    amax = np.abs(w).max(1)
    byte = np.clip(np.where(amax > 0, np.frexp(amax)[1] - 1 + 127 - 7, 1), 1, 254)
    scaled = (w * np.exp2(127.0 - byte)[:, None, :]).reshape(k, n).astype(np.float32)
    words = np.ascontiguousarray(scaled.reshape(k // 512, 128, 4, n).transpose(0, 1, 3, 2)).astype(ml_dtypes.float8_e4m3fn).view(np.uint8)
    return words, np.ascontiguousarray(byte.astype(np.uint8).reshape(k // 512, 16, n))


def unpack_weight(words, scales):
    g, p, n, _ = words.shape
    vals = np.ascontiguousarray(words).view(ml_dtypes.float8_e4m3fn).astype(np.float64) * np.repeat(np.exp2(scales.astype(np.float64) - 127.0), 8, axis=1)[..., None]
    return vals.transpose(0, 1, 3, 2).reshape(g * 512, n)


K, T, S, H, N, V = 1024, 2048, 1024, 512, 128, 512


def setup_inputs():
    n = np.random.standard_normal
    s = mx_kscale(K)[:, None]
    u = mx_kscale(H)
    packed_xT = pack_weight(n((K, T)) * s)
    return {
        "x_words": packed_xT[0],
        "x_scales": packed_xT[1],
        "w1": (n((K, H)) / np.sqrt(K) / s * u).astype(np.float32),
        "w2": (n((H, N)) / np.sqrt(H) / u[:, None]).astype(np.float32),
        "offs": striped8(np.stack([np.random.permutation(T)[:S] for _ in range(8)])),
        "left": striped(np.random.permutation(S)[:V]),
        "right": striped(np.random.permutation(S)[:V]),
    }


def reference(x_words, x_scales, w1, w2, offs, left, right):
    xq = unpack_weight(x_words, x_scales)[np.arange(K)[:, None], runs(offs, K)]
    h = mxq(f64(w1), 0, "e4m3").T @ xq
    z = np.abs(h[:, unstriped(left)] - h[:, unstriped(right)])
    return mxq(f64(w2), 0, "e4m3").T @ mxq(z, 0, "e4m3")

@@ -1,0 +1,197 @@
+from contextlib import ExitStack
+
+import concourse.mybir as mybir
+
+K, T, S, H, N, V = 1024, 2048, 1024, 512, 128, 512
+FLOPS = 2 * K * H * S + 2 * H * N * V
+
+F32 = mybir.dt.float32
+BF16 = mybir.dt.bfloat16
+I32 = mybir.dt.int32
+U32 = mybir.dt.uint32
+U16 = mybir.dt.uint16
+U8 = mybir.dt.uint8
+FP8X4 = mybir.dt.float8_e4m3fn_x4
+ABS = mybir.ActivationFunctionType.Abs
+SUB = mybir.AluOpType.subtract
+
+P = 128
+PASSES = K // 512
+BANK = 512
+CHUNKS = ((0, 256), (256, 384), (384, 512))
+
+
+def tile_picked_phpair_abs_p_kernel(
+    tc, x_words, x_scales, w1, w2, offs, left, right, out
+):
+    nc = tc.nc
+    with ExitStack() as ctx:
+        keep = ctx.enter_context(tc.tile_pool(name="keep", bufs=1))
+        stage = ctx.enter_context(tc.tile_pool(name="stage", bufs=2))
+        psum = ctx.enter_context(tc.psum_pool(name="psum", bufs=1))
+
+        offs_sb = keep.tile([P, S // 16], U16, name="offs_sb")
+        left_sb = keep.tile([P, V // 16], U16, name="left_sb")
+        right_sb = keep.tile([P, V // 16], U16, name="right_sb")
+        nc.sync.dma_start(offs_sb[:], offs)
+        nc.sync.dma_start(left_sb[:], left)
+        nc.sync.dma_start(right_sb[:], right)
+
+        scale_table = keep.tile([P, T], U8, name="scale_table", tag="reused", align_bytes=64)
+        nc.vector.memset(scale_table[:].bitcast(I32), 0)
+        scale_rows = x_scales.rearrange("z (g e) c -> e g z c", e=2)
+        for e in range(2):
+            nc.scalar.dma_start(scale_table[e:P:8, :].bitcast(I32), scale_rows[e].bitcast(I32))
+
+        warm = keep.tile([P, 8], F32, name="warm")
+        warm_out = keep.tile([P, 8], F32, name="warm_out")
+        nc.vector.memset(warm[:], 0.0)
+        nc.scalar.activation(warm_out[:], warm[:], ABS)
+
+        word_table = []
+        w1_raw = []
+        for z in range(PASSES):
+            table = keep.tile([P, T], U32, name="word_table%d" % z, align_bytes=64)
+            nc.sync.dma_start(table[:].bitcast(I32), x_words[z].rearrange("p c r -> p (c r)").bitcast(I32))
+            word_table.append(table)
+            raw = stage.tile([P, 4 * H], F32, name="w_raw", tag="w_raw")
+            nc.sync.dma_start(raw[:], w1[512 * z : 512 * (z + 1), :].rearrange("(p j) c -> p (j c)", j=4))
+            w1_raw.append(raw)
+
+        picked_scales = keep.tile([P, S], U8, name="picked_scales", align_bytes=64)
+        x_plane = keep.tile([P, S], U8, name="x_plane", align_bytes=64)
+        nc.vector.tensor_copy(picked_scales[:], scale_table[:].indirect(offs_sb[:]))
+        nc.vector.tensor_copy(x_plane[:].bitcast(I32), picked_scales[:].bitcast(I32))
+        for z in range(PASSES):
+            for e in range(2):
+                nc.scalar.dma_start(
+                    x_plane[8 * z + 2 + e : P : 32, :].bitcast(I32),
+                    picked_scales[16 + 8 * z + e : P : 32, :].bitcast(I32),
+                )
+
+        banks = {}
+        h = []
+
+        def interleave_w1(copy, z, t):
+            grouped = keep.tile([P, 4 * P], BF16, name="w1_grouped%d%d" % (z, t), align_bytes=64)
+            copy(
+                grouped[:].rearrange("p (b u i j) -> p b u j i", u=2, i=4, j=4),
+                w1_raw[z][:].rearrange("p (j b t u i) -> p t b u j i", j=4, t=4, u=2, i=4)[:, t],
+            )
+            return grouped
+
+        def quantise(grouped, width, name):
+            codes = keep.tile([P, width], U32, name=name + "_codes", align_bytes=64)
+            scales = keep.tile([P, width], U8, name=name + "_scales", align_bytes=64)
+            nc.vector.quantize_mx(out=codes[:].bitcast(FP8X4), scales=scales[:], in_=grouped[:])
+            return codes, scales
+
+        def first_product(z, t, picked, codes, scales):
+            for half in range(S // BANK):
+                cols = slice(half * BANK, (half + 1) * BANK)
+                if z == 0:
+                    banks[t, half] = psum.tile([P, BANK], F32, name="bank%d%d" % (t, half), tag="bank%d%d" % (t, half))
+                nc.tensor.matmul_mx(
+                    out=banks[t, half][:],
+                    lhsT=codes[:].bitcast(FP8X4),
+                    lhsT_scale=scales[:],
+                    rhs=picked[:, cols].bitcast(FP8X4),
+                    rhs_scale=x_plane[8 * z : P, cols],
+                    start=(z == 0),
+                    stop=(z == PASSES - 1),
+                )
+
+        def evacuate(t):
+            row = keep.tile([P, S], F32, name="h%d" % t)
+            for half in range(S // BANK):
+                nc.scalar.copy(row[:, half * BANK : (half + 1) * BANK], banks[t, half][:])
+            h.append(row)
+
+        picked = []
+        picked.append(keep.tile([P, S], U32, name="picked_words0", tag="reused", align_bytes=64))
+        picked.append(keep.tile([P, S], U32, name="picked_words1", align_bytes=64))
+
+        nc.vector.tensor_copy(picked[0][:], word_table[0][:].indirect(offs_sb[:]))
+        for t in range(4):
+            grouped = interleave_w1(nc.scalar.copy, 0, t)
+            codes, scales = quantise(grouped, P, "w1_0%d" % t)
+            first_product(0, t, picked[0], codes, scales)
+
+        nc.vector.tensor_copy(picked[1][:], word_table[1][:].indirect(offs_sb[:]))
+        last_grouped = [
+            interleave_w1(nc.scalar.copy, 1, 0),
+            interleave_w1(nc.vector.tensor_copy, 1, 1),
+            interleave_w1(nc.vector.tensor_copy, 1, 2),
+            interleave_w1(nc.scalar.copy, 1, 3),
+        ]
+        for t in range(4):
+            codes, scales = quantise(last_grouped[t], P, "w1_1%d" % t)
+            first_product(1, t, picked[1], codes, scales)
+            evacuate(t)
+
+        w2_raw = stage.tile([P, 4 * N], F32, name="w_raw", tag="w_raw")
+        w2_rows = w2.rearrange("(b t r) m -> t b r m", t=4, r=8)
+        for t in range(4):
+            nc.sync.dma_start(w2_raw[:, t * N : (t + 1) * N], w2_rows[t])
+        w2_grouped = keep.tile([P, 4 * N], BF16, name="w2_grouped", align_bytes=64)
+        nc.scalar.copy(
+            w2_grouped[:].rearrange("p (c i t) -> p c t i", i=4, t=4),
+            w2_raw[:].rearrange("p (t c i) -> p c t i", t=4, i=4),
+        )
+
+        diffs = []
+        for c, (v0, v1) in enumerate(CHUNKS):
+            diffs.append(keep.tile([P, 4, v1 - v0], F32, name="diff%d" % c))
+        lefts = []
+
+        def subtract(c, t):
+            v0, v1 = CHUNKS[c]
+            nc.vector.tensor_tensor(
+                diffs[c][:, t, :], h[t][:].indirect(right_sb[:, v0 // 16 : v1 // 16]), lefts[t][:, v0:v1], SUB
+            )
+
+        def absolute(c):
+            v0, v1 = CHUNKS[c]
+            z_grouped = keep.tile([P, 4 * (v1 - v0)], BF16, name="z_grouped%d" % c, align_bytes=64)
+            nc.scalar.activation(
+                z_grouped[:].rearrange("p (c i t) -> p c t i", i=4, t=4),
+                diffs[c][:].rearrange("p t (c i) -> p c t i", i=4),
+                ABS,
+            )
+            return z_grouped
+
+        def second_product(c, z_grouped, copy):
+            v0, v1 = CHUNKS[c]
+            codes, scales = quantise(z_grouped, v1 - v0, "z%d" % c)
+            acc = psum.tile([P, v1 - v0], F32, name="acc%d" % c, tag="bank%d0" % c)
+            nc.tensor.matmul_mx(
+                out=acc[:],
+                lhsT=w2_codes[:].bitcast(FP8X4),
+                lhsT_scale=w2_scales[:],
+                rhs=codes[:].bitcast(FP8X4),
+                rhs_scale=scales[:],
+                start=True,
+                stop=True,
+            )
+            result = keep.tile([P, v1 - v0], F32, name="result%d" % c)
+            copy(result[:], acc[:])
+            nc.sync.dma_start(out[:, v0:v1], result[:])
+
+        for t in range(4):
+            fetched = keep.tile([P, V], F32, name="left%d" % t)
+            nc.vector.tensor_copy(fetched[:], h[t][:].indirect(left_sb[:]))
+            lefts.append(fetched)
+            if t > 0:
+                subtract(0, t - 1)
+        subtract(0, 3)
+        w2_codes, w2_scales = quantise(w2_grouped, N, "w2")
+        z0 = absolute(0)
+        for t in range(4):
+            subtract(1, t)
+        z1 = absolute(1)
+        second_product(0, z0, nc.scalar.copy)
+        for t in range(4):
+            subtract(2, t)
+        z2 = absolute(2)
+        second_product(1, z1, nc.scalar.copy)
+        second_product(2, z2, nc.vector.tensor_copy)

@@ -27,7 +27,6 @@ def tile_picked_phpair_abs_p_kernel(
     nc = tc.nc
     with ExitStack() as ctx:
         keep = ctx.enter_context(tc.tile_pool(name="keep", bufs=1))
-        stage = ctx.enter_context(tc.tile_pool(name="stage", bufs=2))
         psum = ctx.enter_context(tc.psum_pool(name="psum", bufs=1))
 
         offs_sb = keep.tile([P, S // 16], U16, name="offs_sb")
@@ -41,33 +40,44 @@ def tile_picked_phpair_abs_p_kernel(
         nc.vector.memset(scale_table[:].bitcast(I32), 0)
         scale_rows = x_scales.rearrange("z (g e) c -> e g z c", e=2)
         for e in range(2):
-            nc.scalar.dma_start(scale_table[e:P:8, :].bitcast(I32), scale_rows[e].bitcast(I32))
+            nc.sync.dma_start(scale_table[e:P:8, :].bitcast(I32), scale_rows[e].bitcast(I32))
 
         warm = keep.tile([P, 8], F32, name="warm")
         warm_out = keep.tile([P, 8], F32, name="warm_out")
         nc.vector.memset(warm[:], 0.0)
         nc.scalar.activation(warm_out[:], warm[:], ABS)
 
+        x_plane = keep.tile([P, S], U8, name="x_plane", align_bytes=64)
+        nc.vector.memset(x_plane[:].bitcast(I32), 0)
+
         word_table = []
         w1_raw = []
-        for z in range(PASSES):
+
+        def load_words(z):
             table = keep.tile([P, T], U32, name="word_table%d" % z, align_bytes=64)
             nc.sync.dma_start(table[:].bitcast(I32), x_words[z].rearrange("p c r -> p (c r)").bitcast(I32))
             word_table.append(table)
-            raw = stage.tile([P, 4 * H], F32, name="w_raw", tag="w_raw")
+
+        def load_w1(z, tag):
+            raw = keep.tile([P, 4 * H], F32, name="w1_raw%d" % z, tag=tag, align_bytes=64)
             nc.sync.dma_start(raw[:], w1[512 * z : 512 * (z + 1), :].rearrange("(p j) c -> p (j c)", j=4))
             w1_raw.append(raw)
 
+        load_words(0)
+        load_words(1)
+        load_w1(0, "w_raw")
+
         picked_scales = keep.tile([P, S], U8, name="picked_scales", align_bytes=64)
-        x_plane = keep.tile([P, S], U8, name="x_plane", align_bytes=64)
         nc.vector.tensor_copy(picked_scales[:], scale_table[:].indirect(offs_sb[:]))
-        nc.vector.tensor_copy(x_plane[:].bitcast(I32), picked_scales[:].bitcast(I32))
+        for e in range(2):
+            nc.sync.dma_start(x_plane[e:P:8, :].bitcast(I32), picked_scales[e:P:8, :].bitcast(I32))
         for z in range(PASSES):
             for e in range(2):
-                nc.scalar.dma_start(
+                nc.sync.dma_start(
                     x_plane[8 * z + 2 + e : P : 32, :].bitcast(I32),
                     picked_scales[16 + 8 * z + e : P : 32, :].bitcast(I32),
                 )
+        load_w1(1, "reused")
 
         banks = {}
         h = []
@@ -90,7 +100,7 @@ def tile_picked_phpair_abs_p_kernel(
             for half in range(S // BANK):
                 cols = slice(half * BANK, (half + 1) * BANK)
                 if z == 0:
-                    banks[t, half] = psum.tile([P, BANK], F32, name="bank%d%d" % (t, half), tag="bank%d%d" % (t, half))
+                    banks[t, half] = psum.tile([P, BANK], F32, name="bank%d%d" % (t, half), tag="bank%d%d" % (t % 2, half))
                 nc.tensor.matmul_mx(
                     out=banks[t, half][:],
                     lhsT=codes[:].bitcast(FP8X4),
@@ -104,32 +114,39 @@ def tile_picked_phpair_abs_p_kernel(
         def evacuate(t):
             row = keep.tile([P, S], F32, name="h%d" % t)
             for half in range(S // BANK):
-                nc.scalar.copy(row[:, half * BANK : (half + 1) * BANK], banks[t, half][:])
+                copy = nc.vector.tensor_copy if (t, half) == (0, 1) else nc.scalar.copy
+                copy(row[:, half * BANK : (half + 1) * BANK], banks[t, half][:])
             h.append(row)
 
         picked = []
-        picked.append(keep.tile([P, S], U32, name="picked_words0", tag="reused", align_bytes=64))
-        picked.append(keep.tile([P, S], U32, name="picked_words1", align_bytes=64))
+        for z in range(PASSES):
+            picked.append(keep.tile([P, S], U32, name="picked_words%d" % z, align_bytes=64))
 
-        nc.vector.tensor_copy(picked[0][:], word_table[0][:].indirect(offs_sb[:]))
+        for z in range(PASSES):
+            nc.vector.tensor_copy(picked[z][:], word_table[z][:].indirect(offs_sb[:]))
+        first = []
         for t in range(4):
-            grouped = interleave_w1(nc.scalar.copy, 0, t)
-            codes, scales = quantise(grouped, P, "w1_0%d" % t)
-            first_product(0, t, picked[0], codes, scales)
+            first.append(quantise(interleave_w1(nc.scalar.copy, 0, t), P, "w1_0%d" % t))
+        for t in range(2):
+            first_product(0, t, picked[0], *first[t])
 
-        nc.vector.tensor_copy(picked[1][:], word_table[1][:].indirect(offs_sb[:]))
+        last = [quantise(interleave_w1(nc.vector.tensor_copy, 1, 0), P, "w1_10")]
+        first_product(1, 0, picked[1], *last[0])
         last_grouped = [
-            interleave_w1(nc.scalar.copy, 1, 0),
-            interleave_w1(nc.vector.tensor_copy, 1, 1),
+            interleave_w1(nc.scalar.copy, 1, 1),
             interleave_w1(nc.vector.tensor_copy, 1, 2),
-            interleave_w1(nc.scalar.copy, 1, 3),
+            interleave_w1(nc.vector.tensor_copy, 1, 3),
         ]
-        for t in range(4):
-            codes, scales = quantise(last_grouped[t], P, "w1_1%d" % t)
-            first_product(1, t, picked[1], codes, scales)
+        for t in range(1, 4):
+            last.append(quantise(last_grouped[t - 1], P, "w1_1%d" % t))
+        evacuate(0)
+        for t in range(1, 4):
+            if t >= 2:
+                first_product(0, t, picked[0], *first[t])
+            first_product(1, t, picked[1], *last[t])
             evacuate(t)
 
-        w2_raw = stage.tile([P, 4 * N], F32, name="w_raw", tag="w_raw")
+        w2_raw = keep.tile([P, 4 * N], F32, name="w2_raw", tag="w_raw", align_bytes=64)
         w2_rows = w2.rearrange("(b t r) m -> t b r m", t=4, r=8)
         for t in range(4):
             nc.sync.dma_start(w2_raw[:, t * N : (t + 1) * N], w2_rows[t])
@@ -163,7 +180,7 @@ def tile_picked_phpair_abs_p_kernel(
         def second_product(c, z_grouped, copy):
             v0, v1 = CHUNKS[c]
             codes, scales = quantise(z_grouped, v1 - v0, "z%d" % c)
-            acc = psum.tile([P, v1 - v0], F32, name="acc%d" % c, tag="bank%d0" % c)
+            acc = psum.tile([P, v1 - v0], F32, name="acc%d" % c, tag="acc%d" % c)
             nc.tensor.matmul_mx(
                 out=acc[:],
                 lhsT=w2_codes[:].bitcast(FP8X4),

@@ -36,19 +36,11 @@ def tile_picked_phpair_abs_p_kernel(
         nc.sync.dma_start(left_sb[:], left)
         nc.sync.dma_start(right_sb[:], right)
 
-        scale_table = keep.tile([P, T], U8, name="scale_table", tag="reused", align_bytes=64)
+        scale_table = keep.tile([P, T], U8, name="scale_table", align_bytes=64)
         nc.vector.memset(scale_table[:].bitcast(I32), 0)
         scale_rows = x_scales.rearrange("z (g e) c -> e g z c", e=2)
         for e in range(2):
             nc.sync.dma_start(scale_table[e:P:8, :].bitcast(I32), scale_rows[e].bitcast(I32))
-
-        warm = keep.tile([P, 8], F32, name="warm")
-        warm_out = keep.tile([P, 8], F32, name="warm_out")
-        nc.vector.memset(warm[:], 0.0)
-        nc.scalar.activation(warm_out[:], warm[:], ABS)
-
-        x_plane = keep.tile([P, S], U8, name="x_plane", align_bytes=64)
-        nc.vector.memset(x_plane[:].bitcast(I32), 0)
 
         word_table = []
         w1_raw = []
@@ -67,28 +59,26 @@ def tile_picked_phpair_abs_p_kernel(
         load_words(1)
         load_w1(0, "w_raw")
 
-        picked_scales = keep.tile([P, S], U8, name="picked_scales", align_bytes=64)
+        picked_scales = keep.tile([P, S], U8, name="picked_scales", tag="reused", align_bytes=64)
+        x_plane = keep.tile([P, S], U8, name="x_plane", align_bytes=64)
         nc.vector.tensor_copy(picked_scales[:], scale_table[:].indirect(offs_sb[:]))
-        for e in range(2):
-            nc.sync.dma_start(x_plane[e:P:8, :].bitcast(I32), picked_scales[e:P:8, :].bitcast(I32))
+        nc.vector.tensor_copy(x_plane[:].bitcast(I32), picked_scales[:].bitcast(I32))
         for z in range(PASSES):
             for e in range(2):
                 nc.sync.dma_start(
                     x_plane[8 * z + 2 + e : P : 32, :].bitcast(I32),
-                    picked_scales[16 + 8 * z + e : P : 32, :].bitcast(I32),
+                    x_plane[16 + 8 * z + e : P : 32, :].bitcast(I32),
                 )
         load_w1(1, "reused")
 
         banks = {}
         h = []
 
-        def interleave_w1(copy, z, t):
-            grouped = keep.tile([P, 4 * P], BF16, name="w1_grouped%d%d" % (z, t), align_bytes=64)
+        def interleave_w1(copy, z, t, grouped):
             copy(
-                grouped[:].rearrange("p (b u i j) -> p b u j i", u=2, i=4, j=4),
+                grouped.rearrange("p (b u i j) -> p b u j i", u=2, i=4, j=4),
                 w1_raw[z][:].rearrange("p (j b t u i) -> p t b u j i", j=4, t=4, u=2, i=4)[:, t],
             )
-            return grouped
 
         def quantise(grouped, width, name):
             codes = keep.tile([P, width], U32, name=name + "_codes", align_bytes=64)
@@ -103,8 +93,8 @@ def tile_picked_phpair_abs_p_kernel(
                     banks[t, half] = psum.tile([P, BANK], F32, name="bank%d%d" % (t, half), tag="bank%d%d" % (t % 2, half))
                 nc.tensor.matmul_mx(
                     out=banks[t, half][:],
-                    lhsT=codes[:].bitcast(FP8X4),
-                    lhsT_scale=scales[:],
+                    lhsT=codes.bitcast(FP8X4),
+                    lhsT_scale=scales,
                     rhs=picked[:, cols].bitcast(FP8X4),
                     rhs_scale=x_plane[8 * z : P, cols],
                     start=(z == 0),
@@ -114,8 +104,7 @@ def tile_picked_phpair_abs_p_kernel(
         def evacuate(t):
             row = keep.tile([P, S], F32, name="h%d" % t)
             for half in range(S // BANK):
-                copy = nc.vector.tensor_copy if (t, half) == (0, 1) else nc.scalar.copy
-                copy(row[:, half * BANK : (half + 1) * BANK], banks[t, half][:])
+                nc.scalar.copy(row[:, half * BANK : (half + 1) * BANK], banks[t, half][:])
             h.append(row)
 
         picked = []
@@ -124,29 +113,35 @@ def tile_picked_phpair_abs_p_kernel(
 
         for z in range(PASSES):
             nc.vector.tensor_copy(picked[z][:], word_table[z][:].indirect(offs_sb[:]))
-        first = []
-        for t in range(4):
-            first.append(quantise(interleave_w1(nc.scalar.copy, 0, t), P, "w1_0%d" % t))
-        for t in range(2):
-            first_product(0, t, picked[0], *first[t])
+        def prepare_w1(copy, z, tiles):
+            name = "w1_%d%d" % (z, tiles[0])
+            tag = "w1_grouped_%d%d" % (z, tiles[0] % 2) if z == 0 else name
+            grouped = keep.tile([P, 4 * P * len(tiles)], BF16, name=name + "_grouped", tag=tag, align_bytes=64)
+            for n, t in enumerate(tiles):
+                interleave_w1(copy, z, t, grouped[:, 4 * P * n : 4 * P * (n + 1)])
+            codes, scales = quantise(grouped, P * len(tiles), name)
+            for n, t in enumerate(tiles):
+                w1_mx[z, t] = (codes[:, P * n : P * (n + 1)], scales[:, P * n : P * (n + 1)])
 
-        last = [quantise(interleave_w1(nc.vector.tensor_copy, 1, 0), P, "w1_10")]
-        first_product(1, 0, picked[1], *last[0])
-        last_grouped = [
-            interleave_w1(nc.scalar.copy, 1, 1),
-            interleave_w1(nc.vector.tensor_copy, 1, 2),
-            interleave_w1(nc.vector.tensor_copy, 1, 3),
-        ]
-        for t in range(1, 4):
-            last.append(quantise(last_grouped[t - 1], P, "w1_1%d" % t))
+        w1_mx = {}
+        prepare_w1(nc.scalar.copy, 0, (0,))
+        first_product(0, 0, picked[0], *w1_mx[0, 0])
+        prepare_w1(nc.scalar.copy, 0, (1,))
+        first_product(0, 1, picked[0], *w1_mx[0, 1])
+        prepare_w1(nc.vector.tensor_copy, 0, (2, 3))
+
+        prepare_w1(nc.vector.tensor_copy, 1, (0,))
+        first_product(1, 0, picked[1], *w1_mx[1, 0])
+        prepare_w1(nc.scalar.copy, 1, (1,))
+        prepare_w1(nc.vector.tensor_copy, 1, (2, 3))
         evacuate(0)
         for t in range(1, 4):
             if t >= 2:
-                first_product(0, t, picked[0], *first[t])
-            first_product(1, t, picked[1], *last[t])
+                first_product(0, t, picked[0], *w1_mx[0, t])
+            first_product(1, t, picked[1], *w1_mx[1, t])
             evacuate(t)
 
-        w2_raw = keep.tile([P, 4 * N], F32, name="w2_raw", tag="w_raw", align_bytes=64)
+        w2_raw = keep.tile([P, 4 * N], F32, name="w2_raw", tag="reused", align_bytes=64)
         w2_rows = w2.rearrange("(b t r) m -> t b r m", t=4, r=8)
         for t in range(4):
             nc.sync.dma_start(w2_raw[:, t * N : (t + 1) * N], w2_rows[t])
@@ -156,30 +151,25 @@ def tile_picked_phpair_abs_p_kernel(
             w2_raw[:].rearrange("p (t c i) -> p c t i", t=4, i=4),
         )
 
-        diffs = []
+        early = keep.tile([P, 3, V], F32, name="early")
+        late = []
+        z_grouped = []
         for c, (v0, v1) in enumerate(CHUNKS):
-            diffs.append(keep.tile([P, 4, v1 - v0], F32, name="diff%d" % c))
+            late.append(keep.tile([P, v1 - v0], F32, name="late%d" % c))
+            z_grouped.append(keep.tile([P, 4 * (v1 - v0)], BF16, name="z_grouped%d" % c, align_bytes=64))
         lefts = []
+        for t in range(4):
+            lefts.append(keep.tile([P, V], F32, name="left%d" % t))
 
-        def subtract(c, t):
-            v0, v1 = CHUNKS[c]
-            nc.vector.tensor_tensor(
-                diffs[c][:, t, :], h[t][:].indirect(right_sb[:, v0 // 16 : v1 // 16]), lefts[t][:, v0:v1], SUB
-            )
+        def fetch_left(t, v0, v1):
+            nc.vector.tensor_copy(lefts[t][:, v0:v1], h[t][:].indirect(left_sb[:, v0 // 16 : v1 // 16]))
 
-        def absolute(c):
-            v0, v1 = CHUNKS[c]
-            z_grouped = keep.tile([P, 4 * (v1 - v0)], BF16, name="z_grouped%d" % c, align_bytes=64)
-            nc.scalar.activation(
-                z_grouped[:].rearrange("p (c i t) -> p c t i", i=4, t=4),
-                diffs[c][:].rearrange("p t (c i) -> p c t i", i=4),
-                ABS,
-            )
-            return z_grouped
+        def subtract(dst, t, v0, v1):
+            nc.vector.tensor_tensor(dst, h[t][:].indirect(right_sb[:, v0 // 16 : v1 // 16]), lefts[t][:, v0:v1], SUB)
 
-        def second_product(c, z_grouped, copy):
+        def second_product(c):
             v0, v1 = CHUNKS[c]
-            codes, scales = quantise(z_grouped, v1 - v0, "z%d" % c)
+            codes, scales = quantise(z_grouped[c], v1 - v0, "z%d" % c)
             acc = psum.tile([P, v1 - v0], F32, name="acc%d" % c, tag="acc%d" % c)
             nc.tensor.matmul_mx(
                 out=acc[:],
@@ -190,25 +180,37 @@ def tile_picked_phpair_abs_p_kernel(
                 start=True,
                 stop=True,
             )
+            return acc
+
+        def store(c, acc, copy):
+            v0, v1 = CHUNKS[c]
             result = keep.tile([P, v1 - v0], F32, name="result%d" % c)
             copy(result[:], acc[:])
             nc.sync.dma_start(out[:, v0:v1], result[:])
 
-        for t in range(4):
-            fetched = keep.tile([P, V], F32, name="left%d" % t)
-            nc.vector.tensor_copy(fetched[:], h[t][:].indirect(left_sb[:]))
-            lefts.append(fetched)
-            if t > 0:
-                subtract(0, t - 1)
-        subtract(0, 3)
+        halves = ((0, V // 2), (V // 2, V))
+        for t in range(3):
+            for v0, v1 in halves:
+                fetch_left(t, v0, v1)
+            for v0, v1 in halves:
+                subtract(early[:, t, v0:v1], t, v0, v1)
         w2_codes, w2_scales = quantise(w2_grouped, N, "w2")
-        z0 = absolute(0)
-        for t in range(4):
-            subtract(1, t)
-        z1 = absolute(1)
-        second_product(0, z0, nc.scalar.copy)
-        for t in range(4):
-            subtract(2, t)
-        z2 = absolute(2)
-        second_product(1, z1, nc.scalar.copy)
-        second_product(2, z2, nc.vector.tensor_copy)
+        for c, (v0, v1) in enumerate(CHUNKS):
+            nc.scalar.activation(
+                z_grouped[c][:].rearrange("p (c i t) -> p c t i", i=4, t=4)[:, :, 0:3, :],
+                early[:, :, v0:v1].rearrange("p t (c i) -> p c t i", i=4),
+                ABS,
+            )
+        accs = []
+        fetch_left(3, *CHUNKS[0])
+        for c, (v0, v1) in enumerate(CHUNKS):
+            if c + 1 < len(CHUNKS):
+                fetch_left(3, *CHUNKS[c + 1])
+            subtract(late[c][:], 3, v0, v1)
+            nc.scalar.activation(z_grouped[c][:].rearrange("p (v t) -> p v t", t=4)[:, :, 3], late[c][:], ABS)
+        accs.append(second_product(0))
+        accs.append(second_product(1))
+        store(0, accs[0], nc.vector.tensor_copy)
+        accs.append(second_product(2))
+        store(1, accs[1], nc.scalar.copy)
+        store(2, accs[2], nc.vector.tensor_copy)

@@ -18,7 +18,8 @@ SUB = mybir.AluOpType.subtract
 P = 128
 PASSES = K // 512
 BANK = 512
-CHUNKS = ((0, 256), (256, 384), (384, 512))
+HALF = H // 2
+CHUNKS = ((0, 256), (256, 384), (384, 448), (448, 512))
 
 
 def tile_picked_phpair_abs_p_kernel(
@@ -36,113 +37,166 @@ def tile_picked_phpair_abs_p_kernel(
         nc.sync.dma_start(left_sb[:], left)
         nc.sync.dma_start(right_sb[:], right)
 
-        scale_table = keep.tile([P, T], U8, name="scale_table", align_bytes=64)
+        scale_table = keep.tile([P, T], U8, name="scale_table", tag="after_scales", align_bytes=64)
+        x_plane = keep.tile([P, S], U8, name="x_plane", align_bytes=64)
         nc.vector.memset(scale_table[:].bitcast(I32), 0)
         scale_rows = x_scales.rearrange("z (g e) c -> e g z c", e=2)
         for e in range(2):
             nc.sync.dma_start(scale_table[e:P:8, :].bitcast(I32), scale_rows[e].bitcast(I32))
 
         word_table = []
-        w1_raw = []
+        w1_raw = {}
 
         def load_words(z):
             table = keep.tile([P, T], U32, name="word_table%d" % z, align_bytes=64)
             nc.sync.dma_start(table[:].bitcast(I32), x_words[z].rearrange("p c r -> p (c r)").bitcast(I32))
             word_table.append(table)
 
-        def load_w1(z, tag):
-            raw = keep.tile([P, 4 * H], F32, name="w1_raw%d" % z, tag=tag, align_bytes=64)
-            nc.sync.dma_start(raw[:], w1[512 * z : 512 * (z + 1), :].rearrange("(p j) c -> p (j c)", j=4))
-            w1_raw.append(raw)
+        def load_w1(z, hf, raw):
+            nc.sync.dma_start(
+                raw.rearrange("p (j c) -> p j c", j=4),
+                w1[512 * z : 512 * (z + 1), HALF * hf : HALF * (hf + 1)].rearrange("(p j) c -> p j c", j=4),
+            )
+            w1_raw[z, hf] = raw
 
         load_words(0)
         load_words(1)
-        load_w1(0, "w_raw")
+        w1_first = keep.tile([P, 4 * HALF], F32, name="w1_first", tag="w1_first", align_bytes=64)
+        load_w1(0, 0, w1_first[:])
 
-        picked_scales = keep.tile([P, S], U8, name="picked_scales", tag="reused", align_bytes=64)
-        x_plane = keep.tile([P, S], U8, name="x_plane", align_bytes=64)
+        picked_scales = keep.tile([P, S], U8, name="picked_scales", align_bytes=64)
         nc.vector.tensor_copy(picked_scales[:], scale_table[:].indirect(offs_sb[:]))
         nc.vector.tensor_copy(x_plane[:].bitcast(I32), picked_scales[:].bitcast(I32))
         for z in range(PASSES):
             for e in range(2):
                 nc.sync.dma_start(
                     x_plane[8 * z + 2 + e : P : 32, :].bitcast(I32),
-                    x_plane[16 + 8 * z + e : P : 32, :].bitcast(I32),
+                    picked_scales[16 + 8 * z + e : P : 32, :].bitcast(I32),
                 )
-        load_w1(1, "reused")
+        w1_rest = keep.tile([P, 3 * 4 * HALF], F32, name="w1_rest", tag="after_scales", align_bytes=64)
+        for n, (z, hf) in enumerate(((1, 0), (0, 1), (1, 1))):
+            load_w1(z, hf, w1_rest[:, 4 * HALF * n : 4 * HALF * (n + 1)])
 
-        banks = {}
-        h = []
+        picked = {}
 
-        def interleave_w1(copy, z, t, grouped):
+        def pick_words(z, s0, s1, tag):
+            words = keep.tile([P, s1 - s0], U32, name="picked%d_%d" % (z, s0), tag=tag, align_bytes=64)
+            nc.vector.tensor_copy(words[:], word_table[z][:].indirect(offs_sb[:, s0 // 16 : s1 // 16]))
+            for half in range(s0 // BANK, s1 // BANK):
+                picked[z, half] = words[:, half * BANK - s0 : (half + 1) * BANK - s0]
+
+        def raw_pair(z, hf, pair):
+            return w1_raw[z, hf].rearrange("p (j g s t e) -> p s t g j e", j=4, s=2, t=2, e=4)[:, pair]
+
+        staging = keep.tile([P, 12 * P], BF16, name="staging", align_bytes=64)
+        grouped = {(0, 2): staging[:, 0 : 8 * P], (1, 0): staging[:, 6 * P : 10 * P], (0, 1): staging[:, 8 * P : 12 * P]}
+        grouped[0, 0] = keep.tile([P, 4 * P], BF16, name="grouped00", tag="grouped00", align_bytes=64)
+        grouped[1, 1] = keep.tile([P, 4 * P], BF16, name="grouped11", tag="left0", align_bytes=64)
+        grouped[1, 2] = keep.tile([P, 8 * P], BF16, name="grouped12", tag="grouped12", align_bytes=64)
+
+        def interleave_own(copy, z, hf):
+            copy(grouped[z, hf][:].rearrange("p (t g e j) -> p t g j e", t=2, e=4, j=4), raw_pair(z, hf, 0))
+
+        def interleave_mixed(copy, z, hf):
             copy(
-                grouped.rearrange("p (b u i j) -> p b u j i", u=2, i=4, j=4),
-                w1_raw[z][:].rearrange("p (j b t u i) -> p t b u j i", j=4, t=4, u=2, i=4)[:, t],
+                grouped[z, 2][:].rearrange("p (t h g e j) -> p h t g j e", t=2, h=2, e=4, j=4)[:, hf],
+                raw_pair(z, hf, 1),
             )
 
-        def quantise(grouped, width, name):
+        def quantise(values, width, name):
             codes = keep.tile([P, width], U32, name=name + "_codes", align_bytes=64)
             scales = keep.tile([P, width], U8, name=name + "_scales", align_bytes=64)
-            nc.vector.quantize_mx(out=codes[:].bitcast(FP8X4), scales=scales[:], in_=grouped[:])
+            nc.vector.quantize_mx(out=codes[:].bitcast(FP8X4), scales=scales[:], in_=values[:])
             return codes, scales
 
-        def first_product(z, t, picked, codes, scales):
+        w1_mx = {}
+
+        def quantise_w1(z, t, count):
+            codes, scales = quantise(grouped[z, t], P * count, "w1_%d%d" % (z, t))
+            for n in range(count):
+                w1_mx[z, t + n] = (codes[:, P * n : P * (n + 1)], scales[:, P * n : P * (n + 1)])
+
+        banks = {}
+
+        def first_product(z, t):
+            codes, scales = w1_mx[z, t]
             for half in range(S // BANK):
-                cols = slice(half * BANK, (half + 1) * BANK)
                 if z == 0:
-                    banks[t, half] = psum.tile([P, BANK], F32, name="bank%d%d" % (t, half), tag="bank%d%d" % (t % 2, half))
+                    banks[t, half] = psum.tile([P, BANK], F32, name="bank%d%d" % (t, half), tag="bank%d%d" % (t, half))
                 nc.tensor.matmul_mx(
                     out=banks[t, half][:],
                     lhsT=codes.bitcast(FP8X4),
                     lhsT_scale=scales,
-                    rhs=picked[:, cols].bitcast(FP8X4),
-                    rhs_scale=x_plane[8 * z : P, cols],
+                    rhs=picked[z, half].bitcast(FP8X4),
+                    rhs_scale=x_plane[8 * z : P, half * BANK : (half + 1) * BANK],
                     start=(z == 0),
                     stop=(z == PASSES - 1),
                 )
 
-        def evacuate(t):
-            row = keep.tile([P, S], F32, name="h%d" % t)
-            for half in range(S // BANK):
-                nc.scalar.copy(row[:, half * BANK : (half + 1) * BANK], banks[t, half][:])
-            h.append(row)
+        h = []
+        for t in range(4):
+            h.append(keep.tile([P, S], F32, name="h%d" % t))
 
-        picked = []
-        for z in range(PASSES):
-            picked.append(keep.tile([P, S], U32, name="picked_words%d" % z, align_bytes=64))
+        def evacuate(t, s0, s1):
+            half = s0 // BANK
+            nc.scalar.copy(h[t][:, s0:s1], banks[t, half][:, s0 - half * BANK : s1 - half * BANK])
 
-        for z in range(PASSES):
-            nc.vector.tensor_copy(picked[z][:], word_table[z][:].indirect(offs_sb[:]))
-        def prepare_w1(copy, z, tiles):
-            name = "w1_%d%d" % (z, tiles[0])
-            tag = "w1_grouped_%d%d" % (z, tiles[0] % 2) if z == 0 else name
-            grouped = keep.tile([P, 4 * P * len(tiles)], BF16, name=name + "_grouped", tag=tag, align_bytes=64)
-            for n, t in enumerate(tiles):
-                interleave_w1(copy, z, t, grouped[:, 4 * P * n : 4 * P * (n + 1)])
-            codes, scales = quantise(grouped, P * len(tiles), name)
-            for n, t in enumerate(tiles):
-                w1_mx[z, t] = (codes[:, P * n : P * (n + 1)], scales[:, P * n : P * (n + 1)])
+        pick_words(0, 0, S, "picked0")
+        pick_words(1, 0, BANK, "picked1")
+        interleave_own(nc.scalar.copy, 0, 0)
+        quantise_w1(0, 0, 1)
+        first_product(0, 0)
+        pick_words(1, BANK, S, "grouped00")
+        interleave_own(nc.scalar.copy, 1, 0)
+        quantise_w1(1, 0, 1)
+        first_product(1, 0)
+        evacuate(0, 0, BANK)
+        evacuate(0, BANK, S)
+        interleave_own(nc.vector.tensor_copy, 0, 1)
+        quantise_w1(0, 1, 1)
+        first_product(0, 1)
+        interleave_mixed(nc.scalar.copy, 0, 0)
+        interleave_mixed(nc.vector.tensor_copy, 0, 1)
+        quantise_w1(0, 2, 2)
+        interleave_own(nc.vector.tensor_copy, 1, 1)
+        quantise_w1(1, 1, 1)
+        first_product(1, 1)
+        interleave_mixed(nc.scalar.copy, 1, 0)
+        interleave_mixed(nc.scalar.copy, 1, 1)
+        quantise_w1(1, 2, 2)
+        evacuate(1, 0, BANK)
+        evacuate(1, BANK, S)
+        for t in (2, 3):
+            first_product(0, t)
+        for t in (2, 3):
+            first_product(1, t)
+        evacuate(2, 0, BANK)
+        evacuate(3, 0, BANK)
+        evacuate(2, BANK, S - 128)
+        evacuate(3, BANK, S)
+        evacuate(2, S - 128, S)
 
-        w1_mx = {}
-        prepare_w1(nc.scalar.copy, 0, (0,))
-        first_product(0, 0, picked[0], *w1_mx[0, 0])
-        prepare_w1(nc.scalar.copy, 0, (1,))
-        first_product(0, 1, picked[0], *w1_mx[0, 1])
-        prepare_w1(nc.vector.tensor_copy, 0, (2, 3))
+        diff = keep.tile([P, 4, V], F32, name="diff", tag="grouped12", align_bytes=64)
+        moving = keep.tile([P, V], F32, name="moving")
+        lefts = []
+        for t in range(4):
+            lefts.append(keep.tile([P, V], F32, name="left%d" % t, tag="left%d" % t, align_bytes=64))
 
-        prepare_w1(nc.vector.tensor_copy, 1, (0,))
-        first_product(1, 0, picked[1], *w1_mx[1, 0])
-        prepare_w1(nc.scalar.copy, 1, (1,))
-        prepare_w1(nc.vector.tensor_copy, 1, (2, 3))
-        evacuate(0)
-        for t in range(1, 4):
-            if t >= 2:
-                first_product(0, t, picked[0], *w1_mx[0, t])
-            first_product(1, t, picked[1], *w1_mx[1, t])
-            evacuate(t)
+        def fetch_left(t, v0, v1):
+            nc.vector.tensor_copy(lefts[t][:, v0:v1], h[t][:].indirect(left_sb[:, v0 // 16 : v1 // 16]))
 
-        w2_raw = keep.tile([P, 4 * N], F32, name="w2_raw", tag="reused", align_bytes=64)
-        w2_rows = w2.rearrange("(b t r) m -> t b r m", t=4, r=8)
+        def subtract(dst, t, v0, v1):
+            nc.vector.tensor_tensor(dst, h[t][:].indirect(right_sb[:, v0 // 16 : v1 // 16]), lefts[t][:, v0:v1], SUB)
+
+        halves = ((0, V // 2), (V // 2, V))
+        for v0, v1 in halves:
+            fetch_left(0, v0, v1)
+        for v0, v1 in halves:
+            subtract(diff[:, 0, v0:v1], 0, v0, v1)
+        nc.sync.dma_start(diff[0:64, 1, :], diff[64:P, 0, :])
+
+        w2_raw = keep.tile([P, 4 * N], F32, name="w2_raw", tag="left0", align_bytes=64)
+        w2_rows = w2.rearrange("(g t e) m -> t g e m", t=4, e=4)
         for t in range(4):
             nc.sync.dma_start(w2_raw[:, t * N : (t + 1) * N], w2_rows[t])
         w2_grouped = keep.tile([P, 4 * N], BF16, name="w2_grouped", align_bytes=64)
@@ -151,26 +205,32 @@ def tile_picked_phpair_abs_p_kernel(
             w2_raw[:].rearrange("p (t c i) -> p c t i", t=4, i=4),
         )
 
-        early = keep.tile([P, 3, V], F32, name="early")
-        late = []
+        for v0, v1 in halves:
+            fetch_left(1, v0, v1)
+        for v0, v1 in halves:
+            subtract(moving[:, v0:v1], 1, v0, v1)
+        nc.sync.dma_start(diff[64:P, 0, :], moving[0:64, :])
+        nc.sync.dma_start(diff[64:P, 1, :], moving[64:P, :])
+
         z_grouped = []
         for c, (v0, v1) in enumerate(CHUNKS):
-            late.append(keep.tile([P, v1 - v0], F32, name="late%d" % c))
+            if v0 % 128 == 0:
+                for t in (3, 2):
+                    fetch_left(t, v0, max(v1, v0 + 128))
+            for t in (3, 2):
+                subtract(diff[:, t, v0:v1], t, v0, v1)
             z_grouped.append(keep.tile([P, 4 * (v1 - v0)], BF16, name="z_grouped%d" % c, align_bytes=64))
-        lefts = []
-        for t in range(4):
-            lefts.append(keep.tile([P, V], F32, name="left%d" % t))
-
-        def fetch_left(t, v0, v1):
-            nc.vector.tensor_copy(lefts[t][:, v0:v1], h[t][:].indirect(left_sb[:, v0 // 16 : v1 // 16]))
-
-        def subtract(dst, t, v0, v1):
-            nc.vector.tensor_tensor(dst, h[t][:].indirect(right_sb[:, v0 // 16 : v1 // 16]), lefts[t][:, v0:v1], SUB)
+            nc.scalar.activation(
+                z_grouped[c][:].rearrange("p (c i t) -> p c t i", i=4, t=4),
+                diff[:, :, v0:v1].rearrange("p t (c i) -> p c t i", i=4),
+                ABS,
+            )
+        w2_codes, w2_scales = quantise(w2_grouped, N, "w2")
 
         def second_product(c):
             v0, v1 = CHUNKS[c]
             codes, scales = quantise(z_grouped[c], v1 - v0, "z%d" % c)
-            acc = psum.tile([P, v1 - v0], F32, name="acc%d" % c, tag="acc%d" % c)
+            acc = psum.tile([P, v1 - v0], F32, name="acc%d" % c, tag="bank%d%d" % (c // 2, c % 2))
             nc.tensor.matmul_mx(
                 out=acc[:],
                 lhsT=w2_codes[:].bitcast(FP8X4),
@@ -188,29 +248,5 @@ def tile_picked_phpair_abs_p_kernel(
             copy(result[:], acc[:])
             nc.sync.dma_start(out[:, v0:v1], result[:])
 
-        halves = ((0, V // 2), (V // 2, V))
-        for t in range(3):
-            for v0, v1 in halves:
-                fetch_left(t, v0, v1)
-            for v0, v1 in halves:
-                subtract(early[:, t, v0:v1], t, v0, v1)
-        w2_codes, w2_scales = quantise(w2_grouped, N, "w2")
-        for c, (v0, v1) in enumerate(CHUNKS):
-            nc.scalar.activation(
-                z_grouped[c][:].rearrange("p (c i t) -> p c t i", i=4, t=4)[:, :, 0:3, :],
-                early[:, :, v0:v1].rearrange("p t (c i) -> p c t i", i=4),
-                ABS,
-            )
-        accs = []
-        fetch_left(3, *CHUNKS[0])
-        for c, (v0, v1) in enumerate(CHUNKS):
-            if c + 1 < len(CHUNKS):
-                fetch_left(3, *CHUNKS[c + 1])
-            subtract(late[c][:], 3, v0, v1)
-            nc.scalar.activation(z_grouped[c][:].rearrange("p (v t) -> p v t", t=4)[:, :, 3], late[c][:], ABS)
-        accs.append(second_product(0))
-        accs.append(second_product(1))
-        store(0, accs[0], nc.vector.tensor_copy)
-        accs.append(second_product(2))
-        store(1, accs[1], nc.scalar.copy)
-        store(2, accs[2], nc.vector.tensor_copy)
+        for c in range(len(CHUNKS)):
+            store(c, second_product(c), nc.vector.tensor_copy if c == len(CHUNKS) - 1 else nc.scalar.copy)

@@ -20,6 +20,7 @@ PASSES = K // 512
 BANK = 512
 HALF = H // 2
 CHUNKS = ((0, 256), (256, 384), (384, 448), (448, 512))
+STORES = ((0,), (1,), (2, 3))
 
 
 def tile_picked_phpair_abs_p_kernel(
@@ -91,8 +92,9 @@ def tile_picked_phpair_abs_p_kernel(
         staging = keep.tile([P, 12 * P], BF16, name="staging", align_bytes=64)
         grouped = {(0, 2): staging[:, 0 : 8 * P], (1, 0): staging[:, 6 * P : 10 * P], (0, 1): staging[:, 8 * P : 12 * P]}
         grouped[0, 0] = keep.tile([P, 4 * P], BF16, name="grouped00", tag="grouped00", align_bytes=64)
-        grouped[1, 1] = keep.tile([P, 4 * P], BF16, name="grouped11", tag="left0", align_bytes=64)
-        grouped[1, 2] = keep.tile([P, 8 * P], BF16, name="grouped12", tag="grouped12", align_bytes=64)
+        staging_last = keep.tile([P, 8 * P], F32, name="staging_last", tag="staging_last", align_bytes=64)
+        grouped[1, 1] = staging_last[:, 3 * P : 5 * P].bitcast(BF16)
+        grouped[1, 2] = staging_last[:, 0 : 4 * P].bitcast(BF16)
 
         def interleave_own(copy, z, hf):
             copy(grouped[z, hf][:].rearrange("p (t g e j) -> p t g j e", t=2, e=4, j=4), raw_pair(z, hf, 0))
@@ -156,61 +158,67 @@ def tile_picked_phpair_abs_p_kernel(
         quantise_w1(0, 1, 1)
         first_product(0, 1)
         interleave_mixed(nc.scalar.copy, 0, 0)
-        interleave_mixed(nc.vector.tensor_copy, 0, 1)
+        interleave_mixed(nc.scalar.copy, 0, 1)
         quantise_w1(0, 2, 2)
+        interleave_mixed(nc.scalar.copy, 1, 0)
         interleave_own(nc.vector.tensor_copy, 1, 1)
         quantise_w1(1, 1, 1)
         first_product(1, 1)
-        interleave_mixed(nc.scalar.copy, 1, 0)
         interleave_mixed(nc.scalar.copy, 1, 1)
         quantise_w1(1, 2, 2)
         evacuate(1, 0, BANK)
         evacuate(1, BANK, S)
+        w2_raw = keep.tile([P, 4 * N], F32, name="w2_raw", tag="w1_first", align_bytes=64)
+        w2_rows = w2.rearrange("(g t e) m -> t g e m", t=4, e=4)
+        for t in range(4):
+            nc.sync.dma_start(w2_raw[:, t * N : (t + 1) * N], w2_rows[t])
+        w2_grouped = staging_last[:, 0 : 2 * N].bitcast(BF16)
+        nc.scalar.copy(
+            w2_grouped[:].rearrange("p (c i t) -> p c t i", i=4, t=4),
+            w2_raw[:].rearrange("p (t c i) -> p c t i", t=4, i=4),
+        )
         for t in (2, 3):
             first_product(0, t)
         for t in (2, 3):
             first_product(1, t)
         evacuate(2, 0, BANK)
         evacuate(3, 0, BANK)
-        evacuate(2, BANK, S - 128)
+        evacuate(2, BANK, S - 64)
         evacuate(3, BANK, S)
-        evacuate(2, S - 128, S)
+        evacuate(2, S - 64, S)
 
-        diff = keep.tile([P, 4, V], F32, name="diff", tag="grouped12", align_bytes=64)
-        moving = keep.tile([P, V], F32, name="moving")
-        lefts = []
-        for t in range(4):
+        diff = keep.tile([P, 4, V], F32, name="diff", tag="after_scales", align_bytes=64)
+        moving = keep.tile([P, V], F32, name="moving", tag="w1_first", align_bytes=64)
+        lefts = [staging_last[:, 4 * P : 8 * P]]
+        for t in range(1, 4):
             lefts.append(keep.tile([P, V], F32, name="left%d" % t, tag="left%d" % t, align_bytes=64))
 
+        left_from = {}
+
         def fetch_left(t, v0, v1):
-            nc.vector.tensor_copy(lefts[t][:, v0:v1], h[t][:].indirect(left_sb[:, v0 // 16 : v1 // 16]))
+            left_from[t] = v0
+            nc.vector.tensor_copy(lefts[t][:, 0 : v1 - v0], h[t][:].indirect(left_sb[:, v0 // 16 : v1 // 16]))
 
         def subtract(dst, t, v0, v1):
-            nc.vector.tensor_tensor(dst, h[t][:].indirect(right_sb[:, v0 // 16 : v1 // 16]), lefts[t][:, v0:v1], SUB)
+            nc.vector.tensor_tensor(
+                dst,
+                h[t][:].indirect(right_sb[:, v0 // 16 : v1 // 16]),
+                lefts[t][:, v0 - left_from[t] : v1 - left_from[t]],
+                SUB,
+            )
 
-        halves = ((0, V // 2), (V // 2, V))
-        for v0, v1 in halves:
-            fetch_left(0, v0, v1)
-        for v0, v1 in halves:
-            subtract(diff[:, 0, v0:v1], 0, v0, v1)
+        fetch_left(0, 0, V)
+        subtract(diff[:, 0, :], 0, 0, V)
         nc.sync.dma_start(diff[0:64, 1, :], diff[64:P, 0, :])
 
-        w2_raw = keep.tile([P, 4 * N], F32, name="w2_raw", tag="left0", align_bytes=64)
-        w2_rows = w2.rearrange("(g t e) m -> t g e m", t=4, e=4)
-        for t in range(4):
-            nc.sync.dma_start(w2_raw[:, t * N : (t + 1) * N], w2_rows[t])
-        w2_grouped = keep.tile([P, 4 * N], BF16, name="w2_grouped", align_bytes=64)
-        nc.scalar.copy(
-            w2_grouped[:].rearrange("p (c i t) -> p c t i", i=4, t=4),
-            w2_raw[:].rearrange("p (t c i) -> p c t i", t=4, i=4),
-        )
-
-        for v0, v1 in halves:
-            fetch_left(1, v0, v1)
-        for v0, v1 in halves:
+        fetch_left(1, 0, V)
+        w2_codes = keep.tile([P, N], U32, name="w2_codes", align_bytes=64)
+        w2_scales = keep.tile([P, N], U8, name="w2_scales", align_bytes=64)
+        nc.vector.quantize_mx(out=w2_codes[:].bitcast(FP8X4), scales=w2_scales[:], in_=w2_grouped[:])
+        for v0, v1 in ((0, V // 2), (V // 2, V)):
             subtract(moving[:, v0:v1], 1, v0, v1)
-        nc.sync.dma_start(diff[64:P, 0, :], moving[0:64, :])
-        nc.sync.dma_start(diff[64:P, 1, :], moving[64:P, :])
+            nc.sync.dma_start(diff[64:P, 0, v0:v1], moving[0:64, v0:v1])
+            nc.sync.dma_start(diff[64:P, 1, v0:v1], moving[64:P, v0:v1])
 
         z_grouped = []
         for c, (v0, v1) in enumerate(CHUNKS):
@@ -225,14 +233,12 @@ def tile_picked_phpair_abs_p_kernel(
                 diff[:, :, v0:v1].rearrange("p t (c i) -> p c t i", i=4),
                 ABS,
             )
-        w2_codes, w2_scales = quantise(w2_grouped, N, "w2")
 
-        def second_product(c):
+        def second_product(c, acc):
             v0, v1 = CHUNKS[c]
             codes, scales = quantise(z_grouped[c], v1 - v0, "z%d" % c)
-            acc = psum.tile([P, v1 - v0], F32, name="acc%d" % c, tag="bank%d%d" % (c // 2, c % 2))
             nc.tensor.matmul_mx(
-                out=acc[:],
+                out=acc,
                 lhsT=w2_codes[:].bitcast(FP8X4),
                 lhsT_scale=w2_scales[:],
                 rhs=codes[:].bitcast(FP8X4),
@@ -240,13 +246,13 @@ def tile_picked_phpair_abs_p_kernel(
                 start=True,
                 stop=True,
             )
-            return acc
 
-        def store(c, acc, copy):
-            v0, v1 = CHUNKS[c]
-            result = keep.tile([P, v1 - v0], F32, name="result%d" % c)
+        for n, group in enumerate(STORES):
+            g0, g1 = CHUNKS[group[0]][0], CHUNKS[group[-1]][1]
+            acc = psum.tile([P, g1 - g0], F32, name="acc%d" % n, tag="bank%d%d" % (n // 2, n % 2))
+            for c in group:
+                second_product(c, acc[:, CHUNKS[c][0] - g0 : CHUNKS[c][1] - g0])
+            result = keep.tile([P, g1 - g0], F32, name="result%d" % n)
+            copy = nc.vector.tensor_copy if n == len(STORES) - 1 else nc.scalar.copy
             copy(result[:], acc[:])
-            nc.sync.dma_start(out[:, v0:v1], result[:])
-
-        for c in range(len(CHUNKS)):
-            store(c, second_product(c), nc.vector.tensor_copy if c == len(CHUNKS) - 1 else nc.scalar.copy)
+            nc.sync.dma_start(out[:, g0:g1], result[:])

@@ -19,6 +19,7 @@ P = 128
 PASSES = K // 512
 BANK = 512
 HALF = H // 2
+SPANS = (((0, 256), (256, 512), (512, 768), (768, 1024)),) + 3 * (((0, 512), (512, 1024)),)
 CHUNKS = ((0, 256), (256, 384), (384, 448), (448, 512))
 STORES = ((0,), (1,), (2, 3))
 
@@ -34,6 +35,10 @@ def tile_picked_phpair_abs_p_kernel(
         offs_sb = keep.tile([P, S // 16], U16, name="offs_sb")
         left_sb = keep.tile([P, V // 16], U16, name="left_sb")
         right_sb = keep.tile([P, V // 16], U16, name="right_sb")
+        w1_first = keep.tile([P, 4 * HALF], F32, name="w1_first", tag="w1_first", align_bytes=64)
+        first_rows = w1[0:512, 0:HALF].rearrange("(p j) c -> p j c", j=4)
+        first_view = w1_first[:].rearrange("p (j c) -> p j c", j=4)
+        nc.sync.dma_start(first_view[:, 0:2, :], first_rows[:, 0:2, :])
         nc.sync.dma_start(offs_sb[:], offs)
         nc.sync.dma_start(left_sb[:], left)
         nc.sync.dma_start(right_sb[:], right)
@@ -62,21 +67,24 @@ def tile_picked_phpair_abs_p_kernel(
 
         load_words(0)
         load_words(1)
-        w1_first = keep.tile([P, 4 * HALF], F32, name="w1_first", tag="w1_first", align_bytes=64)
-        load_w1(0, 0, w1_first[:])
+        nc.sync.dma_start(first_view[:, 2:4, :], first_rows[:, 2:4, :])
+        w1_raw[0, 0] = w1_first[:]
+        w1_next = keep.tile([P, 4 * HALF], F32, name="w1_next", align_bytes=64)
+        load_w1(1, 0, w1_next[:])
 
-        picked_scales = keep.tile([P, S], U8, name="picked_scales", align_bytes=64)
+        picked_scales = keep.tile([P, S], U8, name="picked_scales", tag="after_plane", align_bytes=64)
         nc.vector.tensor_copy(picked_scales[:], scale_table[:].indirect(offs_sb[:]))
         nc.vector.tensor_copy(x_plane[:].bitcast(I32), picked_scales[:].bitcast(I32))
         for z in range(PASSES):
             for e in range(2):
                 nc.sync.dma_start(
                     x_plane[8 * z + 2 + e : P : 32, :].bitcast(I32),
-                    picked_scales[16 + 8 * z + e : P : 32, :].bitcast(I32),
+                    x_plane[16 + 8 * z + e : P : 32, :].bitcast(I32),
                 )
-        w1_rest = keep.tile([P, 3 * 4 * HALF], F32, name="w1_rest", tag="after_scales", align_bytes=64)
-        for n, (z, hf) in enumerate(((1, 0), (0, 1), (1, 1))):
-            load_w1(z, hf, w1_rest[:, 4 * HALF * n : 4 * HALF * (n + 1)])
+        w1_third = keep.tile([P, 4 * HALF], F32, name="w1_third", tag="after_scales", align_bytes=64)
+        load_w1(0, 1, w1_third[:])
+        w1_last = keep.tile([P, 4 * HALF], F32, name="w1_last", tag="after_plane", align_bytes=64)
+        load_w1(1, 1, w1_last[:])
 
         picked = {}
 
@@ -89,12 +97,12 @@ def tile_picked_phpair_abs_p_kernel(
         def raw_pair(z, hf, pair):
             return w1_raw[z, hf].rearrange("p (j g s t e) -> p s t g j e", j=4, s=2, t=2, e=4)[:, pair]
 
-        staging = keep.tile([P, 12 * P], BF16, name="staging", align_bytes=64)
-        grouped = {(0, 2): staging[:, 0 : 8 * P], (1, 0): staging[:, 6 * P : 10 * P], (0, 1): staging[:, 8 * P : 12 * P]}
+        staging = keep.tile([P, 6 * P], BF16, name="staging", align_bytes=64)
+        grouped = {(1, 0): staging[:, 0 : 4 * P], (0, 1): staging[:, 2 * P : 6 * P]}
         grouped[0, 0] = keep.tile([P, 4 * P], BF16, name="grouped00", tag="grouped00", align_bytes=64)
-        staging_last = keep.tile([P, 8 * P], F32, name="staging_last", tag="staging_last", align_bytes=64)
-        grouped[1, 1] = staging_last[:, 3 * P : 5 * P].bitcast(BF16)
-        grouped[1, 2] = staging_last[:, 0 : 4 * P].bitcast(BF16)
+        grouped[1, 1] = keep.tile([P, 4 * P], BF16, name="grouped11", tag="left0", align_bytes=64)
+        grouped[0, 2] = keep.tile([P, 8 * P], BF16, name="grouped02", align_bytes=64)
+        grouped[1, 2] = keep.tile([P, 8 * P], BF16, name="grouped12", align_bytes=64)
 
         def interleave_own(copy, z, hf):
             copy(grouped[z, hf][:].rearrange("p (t g e j) -> p t g j e", t=2, e=4, j=4), raw_pair(z, hf, 0))
@@ -122,26 +130,25 @@ def tile_picked_phpair_abs_p_kernel(
 
         def first_product(z, t):
             codes, scales = w1_mx[z, t]
-            for half in range(S // BANK):
+            for n, (s0, s1) in enumerate(SPANS[t]):
+                half = s0 // BANK
                 if z == 0:
-                    banks[t, half] = psum.tile([P, BANK], F32, name="bank%d%d" % (t, half), tag="bank%d%d" % (t, half))
+                    banks[t, s0] = psum.tile([P, s1 - s0], F32, name="bank%d_%d" % (t, s0), tag="bank%d" % ((2 * t + n + 2 * (t > 0)) % 8))
                 nc.tensor.matmul_mx(
-                    out=banks[t, half][:],
+                    out=banks[t, s0][:],
                     lhsT=codes.bitcast(FP8X4),
                     lhsT_scale=scales,
-                    rhs=picked[z, half].bitcast(FP8X4),
-                    rhs_scale=x_plane[8 * z : P, half * BANK : (half + 1) * BANK],
+                    rhs=picked[z, half][:, s0 - half * BANK : s1 - half * BANK].bitcast(FP8X4),
+                    rhs_scale=x_plane[8 * z : P, s0:s1],
                     start=(z == 0),
                     stop=(z == PASSES - 1),
                 )
 
-        h = []
-        for t in range(4):
-            h.append(keep.tile([P, S], F32, name="h%d" % t))
+        h = {}
 
-        def evacuate(t, s0, s1):
-            half = s0 // BANK
-            nc.scalar.copy(h[t][:, s0:s1], banks[t, half][:, s0 - half * BANK : s1 - half * BANK])
+        def evacuate(t, s0, s1, copy=nc.scalar.copy):
+            start = max(a for a, b in SPANS[t] if a <= s0)
+            copy(h[t][:, s0:s1], banks[t, start][:, s0 - start : s1 - start])
 
         pick_words(0, 0, S, "picked0")
         pick_words(1, 0, BANK, "picked1")
@@ -152,45 +159,39 @@ def tile_picked_phpair_abs_p_kernel(
         interleave_own(nc.scalar.copy, 1, 0)
         quantise_w1(1, 0, 1)
         first_product(1, 0)
-        evacuate(0, 0, BANK)
-        evacuate(0, BANK, S)
+        interleave_mixed(nc.scalar.copy, 0, 0)
+        interleave_mixed(nc.scalar.copy, 1, 0)
+        interleave_mixed(nc.scalar.copy, 0, 1)
         interleave_own(nc.vector.tensor_copy, 0, 1)
+        h[0] = keep.tile([P, S], F32, name="h0", tag="after_scales", align_bytes=64)
+        for t in range(1, 4):
+            h[t] = keep.tile([P, S], F32, name="h%d" % t)
+        for s0, s1 in SPANS[0]:
+            evacuate(0, s0, s1)
+        interleave_own(nc.vector.tensor_copy, 1, 1)
         quantise_w1(0, 1, 1)
         first_product(0, 1)
-        interleave_mixed(nc.scalar.copy, 0, 0)
-        interleave_mixed(nc.scalar.copy, 0, 1)
+        interleave_mixed(nc.vector.tensor_copy, 1, 1)
         quantise_w1(0, 2, 2)
-        interleave_mixed(nc.scalar.copy, 1, 0)
-        interleave_own(nc.vector.tensor_copy, 1, 1)
         quantise_w1(1, 1, 1)
         first_product(1, 1)
-        interleave_mixed(nc.scalar.copy, 1, 1)
         quantise_w1(1, 2, 2)
+
         evacuate(1, 0, BANK)
         evacuate(1, BANK, S)
-        w2_raw = keep.tile([P, 4 * N], F32, name="w2_raw", tag="w1_first", align_bytes=64)
-        w2_rows = w2.rearrange("(g t e) m -> t g e m", t=4, e=4)
-        for t in range(4):
-            nc.sync.dma_start(w2_raw[:, t * N : (t + 1) * N], w2_rows[t])
-        w2_grouped = staging_last[:, 0 : 2 * N].bitcast(BF16)
-        nc.scalar.copy(
-            w2_grouped[:].rearrange("p (c i t) -> p c t i", i=4, t=4),
-            w2_raw[:].rearrange("p (t c i) -> p c t i", t=4, i=4),
-        )
         for t in (2, 3):
-            first_product(0, t)
-        for t in (2, 3):
-            first_product(1, t)
+            for z in range(PASSES):
+                first_product(z, t)
         evacuate(2, 0, BANK)
-        evacuate(3, 0, BANK)
         evacuate(2, BANK, S - 64)
+        evacuate(3, 0, BANK)
         evacuate(3, BANK, S)
         evacuate(2, S - 64, S)
 
-        diff = keep.tile([P, 4, V], F32, name="diff", tag="after_scales", align_bytes=64)
-        moving = keep.tile([P, V], F32, name="moving", tag="w1_first", align_bytes=64)
-        lefts = [staging_last[:, 4 * P : 8 * P]]
-        for t in range(1, 4):
+        diff = keep.tile([P, 4, V], F32, name="diff")
+        moving = keep.tile([P, V], F32, name="moving")
+        lefts = []
+        for t in range(4):
             lefts.append(keep.tile([P, V], F32, name="left%d" % t, tag="left%d" % t, align_bytes=64))
 
         left_from = {}
@@ -199,24 +200,35 @@ def tile_picked_phpair_abs_p_kernel(
             left_from[t] = v0
             nc.vector.tensor_copy(lefts[t][:, 0 : v1 - v0], h[t][:].indirect(left_sb[:, v0 // 16 : v1 // 16]))
 
-        def subtract(dst, t, v0, v1):
+        def subtract(dst, values, t, v0, v1):
             nc.vector.tensor_tensor(
                 dst,
                 h[t][:].indirect(right_sb[:, v0 // 16 : v1 // 16]),
-                lefts[t][:, v0 - left_from[t] : v1 - left_from[t]],
+                values,
                 SUB,
             )
 
-        fetch_left(0, 0, V)
-        subtract(diff[:, 0, :], 0, 0, V)
+        halves = ((0, V // 2), (V // 2, V))
+        for v0, v1 in halves:
+            nc.vector.tensor_copy(lefts[0][:, v0:v1], h[0][:].indirect(left_sb[:, v0 // 16 : v1 // 16]))
+        for v0, v1 in halves:
+            subtract(diff[:, 0, v0:v1], lefts[0][:, v0:v1], 0, v0, v1)
         nc.sync.dma_start(diff[0:64, 1, :], diff[64:P, 0, :])
 
-        fetch_left(1, 0, V)
-        w2_codes = keep.tile([P, N], U32, name="w2_codes", align_bytes=64)
-        w2_scales = keep.tile([P, N], U8, name="w2_scales", align_bytes=64)
-        nc.vector.quantize_mx(out=w2_codes[:].bitcast(FP8X4), scales=w2_scales[:], in_=w2_grouped[:])
-        for v0, v1 in ((0, V // 2), (V // 2, V)):
-            subtract(moving[:, v0:v1], 1, v0, v1)
+        w2_raw = keep.tile([P, 4 * N], F32, name="w2_raw", tag="left0", align_bytes=64)
+        w2_rows = w2.rearrange("(g t e) m -> t g e m", t=4, e=4)
+        for t in range(4):
+            nc.sync.dma_start(w2_raw[:, t * N : (t + 1) * N], w2_rows[t])
+        w2_grouped = keep.tile([P, 4 * N], BF16, name="w2_grouped", align_bytes=64)
+        nc.scalar.copy(
+            w2_grouped[:].rearrange("p (c i t) -> p c t i", i=4, t=4),
+            w2_raw[:].rearrange("p (t c i) -> p c t i", t=4, i=4),
+        )
+
+        for v0, v1 in halves:
+            nc.vector.tensor_copy(lefts[1][:, v0:v1], h[1][:].indirect(left_sb[:, v0 // 16 : v1 // 16]))
+        for v0, v1 in halves:
+            subtract(moving[:, v0:v1], lefts[1][:, v0:v1], 1, v0, v1)
             nc.sync.dma_start(diff[64:P, 0, v0:v1], moving[0:64, v0:v1])
             nc.sync.dma_start(diff[64:P, 1, v0:v1], moving[64:P, v0:v1])
 
@@ -226,7 +238,7 @@ def tile_picked_phpair_abs_p_kernel(
                 for t in (3, 2):
                     fetch_left(t, v0, max(v1, v0 + 128))
             for t in (3, 2):
-                subtract(diff[:, t, v0:v1], t, v0, v1)
+                subtract(diff[:, t, v0:v1], lefts[t][:, v0 - left_from[t] : v1 - left_from[t]], t, v0, v1)
             z_grouped.append(keep.tile([P, 4 * (v1 - v0)], BF16, name="z_grouped%d" % c, align_bytes=64))
             nc.scalar.activation(
                 z_grouped[c][:].rearrange("p (c i t) -> p c t i", i=4, t=4),
@@ -234,9 +246,14 @@ def tile_picked_phpair_abs_p_kernel(
                 ABS,
             )
 
+        w2_codes, w2_scales = quantise(w2_grouped, N, "w2")
+        z_codes = keep.tile([P, V], U32, name="z_codes", tag="left3", align_bytes=64)
+        z_scales = keep.tile([P, V], U8, name="z_scales", align_bytes=64)
+
         def second_product(c, acc):
             v0, v1 = CHUNKS[c]
-            codes, scales = quantise(z_grouped[c], v1 - v0, "z%d" % c)
+            codes, scales = z_codes[:, v0:v1], z_scales[:, v0:v1]
+            nc.vector.quantize_mx(out=codes.bitcast(FP8X4), scales=scales, in_=z_grouped[c][:])
             nc.tensor.matmul_mx(
                 out=acc,
                 lhsT=w2_codes[:].bitcast(FP8X4),
@@ -249,7 +266,7 @@ def tile_picked_phpair_abs_p_kernel(
 
         for n, group in enumerate(STORES):
             g0, g1 = CHUNKS[group[0]][0], CHUNKS[group[-1]][1]
-            acc = psum.tile([P, g1 - g0], F32, name="acc%d" % n, tag="bank%d%d" % (n // 2, n % 2))
+            acc = psum.tile([P, g1 - g0], F32, name="acc%d" % n, tag="bank%d" % (2 + n))
             for c in group:
                 second_product(c, acc[:, CHUNKS[c][0] - g0 : CHUNKS[c][1] - g0])
             result = keep.tile([P, g1 - g0], F32, name="result%d" % n)

@@ -46,6 +46,7 @@ def tile_picked_phpair_abs_p_kernel(
         scale_table = keep.tile([P, T], U8, name="scale_table", tag="after_scales", align_bytes=64)
         x_plane = keep.tile([P, S], U8, name="x_plane", align_bytes=64)
         nc.vector.memset(scale_table[:].bitcast(I32), 0)
+        nc.vector.memset(x_plane[:].bitcast(I32), 0)
         scale_rows = x_scales.rearrange("z (g e) c -> e g z c", e=2)
         for e in range(2):
             nc.sync.dma_start(scale_table[e:P:8, :].bitcast(I32), scale_rows[e].bitcast(I32))
@@ -54,7 +55,7 @@ def tile_picked_phpair_abs_p_kernel(
         w1_raw = {}
 
         def load_words(z):
-            table = keep.tile([P, T], U32, name="word_table%d" % z, align_bytes=64)
+            table = keep.tile([P, T], U32, name="word_table%d" % z, tag="word_table%d" % z, align_bytes=64)
             nc.sync.dma_start(table[:].bitcast(I32), x_words[z].rearrange("p c r -> p (c r)").bitcast(I32))
             word_table.append(table)
 
@@ -72,19 +73,18 @@ def tile_picked_phpair_abs_p_kernel(
         w1_next = keep.tile([P, 4 * HALF], F32, name="w1_next", align_bytes=64)
         load_w1(1, 0, w1_next[:])
 
-        picked_scales = keep.tile([P, S], U8, name="picked_scales", tag="after_plane", align_bytes=64)
+        picked_scales = keep.tile([P, S], U8, name="picked_scales", align_bytes=64)
         nc.vector.tensor_copy(picked_scales[:], scale_table[:].indirect(offs_sb[:]))
-        nc.vector.tensor_copy(x_plane[:].bitcast(I32), picked_scales[:].bitcast(I32))
+        for e in range(2):
+            nc.sync.dma_start(x_plane[e:P:8, :].bitcast(I32), picked_scales[e:P:8, :].bitcast(I32))
         for z in range(PASSES):
             for e in range(2):
                 nc.sync.dma_start(
                     x_plane[8 * z + 2 + e : P : 32, :].bitcast(I32),
-                    x_plane[16 + 8 * z + e : P : 32, :].bitcast(I32),
+                    picked_scales[16 + 8 * z + e : P : 32, :].bitcast(I32),
                 )
         w1_third = keep.tile([P, 4 * HALF], F32, name="w1_third", tag="after_scales", align_bytes=64)
         load_w1(0, 1, w1_third[:])
-        w1_last = keep.tile([P, 4 * HALF], F32, name="w1_last", tag="after_plane", align_bytes=64)
-        load_w1(1, 1, w1_last[:])
 
         picked = {}
 
@@ -97,8 +97,9 @@ def tile_picked_phpair_abs_p_kernel(
         def raw_pair(z, hf, pair):
             return w1_raw[z, hf].rearrange("p (j g s t e) -> p s t g j e", j=4, s=2, t=2, e=4)[:, pair]
 
-        staging = keep.tile([P, 6 * P], BF16, name="staging", align_bytes=64)
-        grouped = {(1, 0): staging[:, 0 : 4 * P], (0, 1): staging[:, 2 * P : 6 * P]}
+        grouped = {}
+        grouped[1, 0] = keep.tile([P, 4 * P], BF16, name="grouped10", align_bytes=64)
+        grouped[0, 1] = keep.tile([P, 4 * P], BF16, name="grouped01", align_bytes=64)
         grouped[0, 0] = keep.tile([P, 4 * P], BF16, name="grouped00", tag="grouped00", align_bytes=64)
         grouped[1, 1] = keep.tile([P, 4 * P], BF16, name="grouped11", tag="left0", align_bytes=64)
         grouped[0, 2] = keep.tile([P, 8 * P], BF16, name="grouped02", align_bytes=64)
@@ -151,6 +152,8 @@ def tile_picked_phpair_abs_p_kernel(
             copy(h[t][:, s0:s1], banks[t, start][:, s0 - start : s1 - start])
 
         pick_words(0, 0, S, "picked0")
+        w1_last = keep.tile([P, 4 * HALF], F32, name="w1_last", tag="word_table0", align_bytes=64)
+        load_w1(1, 1, w1_last[:])
         pick_words(1, 0, BANK, "picked1")
         interleave_own(nc.scalar.copy, 0, 0)
         quantise_w1(0, 0, 1)
@@ -161,8 +164,8 @@ def tile_picked_phpair_abs_p_kernel(
         first_product(1, 0)
         interleave_mixed(nc.scalar.copy, 0, 0)
         interleave_mixed(nc.scalar.copy, 1, 0)
+        interleave_own(nc.scalar.copy, 0, 1)
         interleave_mixed(nc.scalar.copy, 0, 1)
-        interleave_own(nc.vector.tensor_copy, 0, 1)
         h[0] = keep.tile([P, S], F32, name="h0", tag="after_scales", align_bytes=64)
         for t in range(1, 4):
             h[t] = keep.tile([P, S], F32, name="h%d" % t)

@@ -16,12 +16,17 @@ ABS = mybir.ActivationFunctionType.Abs
 SUB = mybir.AluOpType.subtract
 
 P = 128
+LOW = P // 2
 PASSES = K // 512
 BANK = 512
+BANKS = 8
 HALF = H // 2
+LIST = 16
 SPANS = (((0, 256), (256, 512), (512, 768), (768, 1024)),) + 3 * (((0, 512), (512, 1024)),)
 CHUNKS = ((0, 256), (256, 384), (384, 448), (448, 512))
+LEFT_MIN = 128
 STORES = ((0,), (1,), (2, 3))
+LAST_COPY = 64
 
 
 def tile_picked_phpair_abs_p_kernel(
@@ -32,9 +37,10 @@ def tile_picked_phpair_abs_p_kernel(
         keep = ctx.enter_context(tc.tile_pool(name="keep", bufs=1))
         psum = ctx.enter_context(tc.psum_pool(name="psum", bufs=1))
 
-        offs_sb = keep.tile([P, S // 16], U16, name="offs_sb")
-        left_sb = keep.tile([P, V // 16], U16, name="left_sb")
-        right_sb = keep.tile([P, V // 16], U16, name="right_sb")
+        offs_sb = keep.tile([P, S // LIST], U16, name="offs_sb")
+        left_sb = keep.tile([P, V // LIST], U16, name="left_sb")
+        right_sb = keep.tile([P, V // LIST], U16, name="right_sb")
+
         w1_first = keep.tile([P, 4 * HALF], F32, name="w1_first", tag="w1_first", align_bytes=64)
         first_rows = w1[0:512, 0:HALF].rearrange("(p j) c -> p j c", j=4)
         first_view = w1_first[:].rearrange("p (j c) -> p j c", j=4)
@@ -47,31 +53,28 @@ def tile_picked_phpair_abs_p_kernel(
         x_plane = keep.tile([P, S], U8, name="x_plane", align_bytes=64)
         nc.vector.memset(scale_table[:].bitcast(I32), 0)
         nc.vector.memset(x_plane[:].bitcast(I32), 0)
-        scale_rows = x_scales.rearrange("z (g e) c -> e g z c", e=2)
+        scale_rows = x_scales.rearrange("z (r e) c -> e r z c", e=2)
         for e in range(2):
             nc.sync.dma_start(scale_table[e:P:8, :].bitcast(I32), scale_rows[e].bitcast(I32))
 
         word_table = []
-        w1_raw = {}
-
-        def load_words(z):
+        for z in range(PASSES):
             table = keep.tile([P, T], U32, name="word_table%d" % z, tag="word_table%d" % z, align_bytes=64)
             nc.sync.dma_start(table[:].bitcast(I32), x_words[z].rearrange("p c r -> p (c r)").bitcast(I32))
             word_table.append(table)
+        nc.sync.dma_start(first_view[:, 2:4, :], first_rows[:, 2:4, :])
 
-        def load_w1(z, hf, raw):
+        w1_raw = {(0, 0): w1_first}
+
+        def load_w1(z, hf, tag):
+            raw = keep.tile([P, 4 * HALF], F32, name="w1_raw%d%d" % (z, hf), tag=tag, align_bytes=64)
             nc.sync.dma_start(
-                raw.rearrange("p (j c) -> p j c", j=4),
+                raw[:].rearrange("p (j c) -> p j c", j=4),
                 w1[512 * z : 512 * (z + 1), HALF * hf : HALF * (hf + 1)].rearrange("(p j) c -> p j c", j=4),
             )
             w1_raw[z, hf] = raw
 
-        load_words(0)
-        load_words(1)
-        nc.sync.dma_start(first_view[:, 2:4, :], first_rows[:, 2:4, :])
-        w1_raw[0, 0] = w1_first[:]
-        w1_next = keep.tile([P, 4 * HALF], F32, name="w1_next", align_bytes=64)
-        load_w1(1, 0, w1_next[:])
+        load_w1(1, 0, "w1_next")
 
         picked_scales = keep.tile([P, S], U8, name="picked_scales", align_bytes=64)
         nc.vector.tensor_copy(picked_scales[:], scale_table[:].indirect(offs_sb[:]))
@@ -83,35 +86,33 @@ def tile_picked_phpair_abs_p_kernel(
                     x_plane[8 * z + 2 + e : P : 32, :].bitcast(I32),
                     picked_scales[16 + 8 * z + e : P : 32, :].bitcast(I32),
                 )
-        w1_third = keep.tile([P, 4 * HALF], F32, name="w1_third", tag="after_scales", align_bytes=64)
-        load_w1(0, 1, w1_third[:])
+        load_w1(0, 1, "after_scales")
 
         picked = {}
 
         def pick_words(z, s0, s1, tag):
             words = keep.tile([P, s1 - s0], U32, name="picked%d_%d" % (z, s0), tag=tag, align_bytes=64)
-            nc.vector.tensor_copy(words[:], word_table[z][:].indirect(offs_sb[:, s0 // 16 : s1 // 16]))
-            for half in range(s0 // BANK, s1 // BANK):
-                picked[z, half] = words[:, half * BANK - s0 : (half + 1) * BANK - s0]
+            nc.vector.tensor_copy(words[:], word_table[z][:].indirect(offs_sb[:, s0 // LIST : s1 // LIST]))
+            for n in range(s0 // BANK, s1 // BANK):
+                picked[z, n] = words[:, n * BANK - s0 : (n + 1) * BANK - s0]
 
-        def raw_pair(z, hf, pair):
-            return w1_raw[z, hf].rearrange("p (j g s t e) -> p s t g j e", j=4, s=2, t=2, e=4)[:, pair]
-
-        grouped = {}
-        grouped[1, 0] = keep.tile([P, 4 * P], BF16, name="grouped10", align_bytes=64)
-        grouped[0, 1] = keep.tile([P, 4 * P], BF16, name="grouped01", align_bytes=64)
+        staging = keep.tile([P, 6 * P], BF16, name="staging", align_bytes=64)
+        grouped = {(1, 0): staging[:, 0 : 4 * P], (0, 1): staging[:, 2 * P : 6 * P]}
         grouped[0, 0] = keep.tile([P, 4 * P], BF16, name="grouped00", tag="grouped00", align_bytes=64)
         grouped[1, 1] = keep.tile([P, 4 * P], BF16, name="grouped11", tag="left0", align_bytes=64)
         grouped[0, 2] = keep.tile([P, 8 * P], BF16, name="grouped02", align_bytes=64)
         grouped[1, 2] = keep.tile([P, 8 * P], BF16, name="grouped12", align_bytes=64)
 
+        def plane_pair(z, hf, pair):
+            return w1_raw[z, hf][:].rearrange("p (j g s t e) -> p s t g j e", j=4, s=2, t=2, e=4)[:, pair]
+
         def interleave_own(copy, z, hf):
-            copy(grouped[z, hf][:].rearrange("p (t g e j) -> p t g j e", t=2, e=4, j=4), raw_pair(z, hf, 0))
+            copy(grouped[z, hf][:].rearrange("p (t g e j) -> p t g j e", t=2, e=4, j=4), plane_pair(z, hf, 0))
 
         def interleave_mixed(copy, z, hf):
             copy(
                 grouped[z, 2][:].rearrange("p (t h g e j) -> p h t g j e", t=2, h=2, e=4, j=4)[:, hf],
-                raw_pair(z, hf, 1),
+                plane_pair(z, hf, 1),
             )
 
         def quantise(values, width, name):
@@ -122,24 +123,25 @@ def tile_picked_phpair_abs_p_kernel(
 
         w1_mx = {}
 
-        def quantise_w1(z, t, count):
-            codes, scales = quantise(grouped[z, t], P * count, "w1_%d%d" % (z, t))
-            for n in range(count):
+        def quantise_w1(z, t, tiles):
+            codes, scales = quantise(grouped[z, t], P * tiles, "w1_%d%d" % (z, t))
+            for n in range(tiles):
                 w1_mx[z, t + n] = (codes[:, P * n : P * (n + 1)], scales[:, P * n : P * (n + 1)])
 
         banks = {}
 
         def first_product(z, t):
             codes, scales = w1_mx[z, t]
+            dealt = sum(len(spans) for spans in SPANS[:t])
             for n, (s0, s1) in enumerate(SPANS[t]):
-                half = s0 // BANK
                 if z == 0:
-                    banks[t, s0] = psum.tile([P, s1 - s0], F32, name="bank%d_%d" % (t, s0), tag="bank%d" % ((2 * t + n + 2 * (t > 0)) % 8))
+                    tag = "bank%d" % ((dealt + n) % BANKS)
+                    banks[t, s0] = psum.tile([P, s1 - s0], F32, name="bank%d_%d" % (t, s0), tag=tag)
                 nc.tensor.matmul_mx(
                     out=banks[t, s0][:],
                     lhsT=codes.bitcast(FP8X4),
                     lhsT_scale=scales,
-                    rhs=picked[z, half][:, s0 - half * BANK : s1 - half * BANK].bitcast(FP8X4),
+                    rhs=picked[z, s0 // BANK][:, s0 % BANK : s0 % BANK + s1 - s0].bitcast(FP8X4),
                     rhs_scale=x_plane[8 * z : P, s0:s1],
                     start=(z == 0),
                     stop=(z == PASSES - 1),
@@ -147,24 +149,24 @@ def tile_picked_phpair_abs_p_kernel(
 
         h = {}
 
-        def evacuate(t, s0, s1, copy=nc.scalar.copy):
+        def evacuate(t, s0, s1):
             start = max(a for a, b in SPANS[t] if a <= s0)
-            copy(h[t][:, s0:s1], banks[t, start][:, s0 - start : s1 - start])
+            nc.scalar.copy(h[t][:, s0:s1], banks[t, start][:, s0 - start : s1 - start])
 
         pick_words(0, 0, S, "picked0")
-        w1_last = keep.tile([P, 4 * HALF], F32, name="w1_last", tag="word_table0", align_bytes=64)
-        load_w1(1, 1, w1_last[:])
+        load_w1(1, 1, "word_table0")
         pick_words(1, 0, BANK, "picked1")
         interleave_own(nc.scalar.copy, 0, 0)
         quantise_w1(0, 0, 1)
         first_product(0, 0)
-        pick_words(1, BANK, S, "grouped00")
+        interleave_mixed(nc.scalar.copy, 0, 0)
+        pick_words(1, BANK, S, "w1_first")
         interleave_own(nc.scalar.copy, 1, 0)
         quantise_w1(1, 0, 1)
         first_product(1, 0)
-        interleave_mixed(nc.scalar.copy, 0, 0)
+
         interleave_mixed(nc.scalar.copy, 1, 0)
-        interleave_own(nc.scalar.copy, 0, 1)
+        interleave_own(nc.vector.tensor_copy, 0, 1)
         interleave_mixed(nc.scalar.copy, 0, 1)
         h[0] = keep.tile([P, S], F32, name="h0", tag="after_scales", align_bytes=64)
         for t in range(1, 4):
@@ -174,49 +176,38 @@ def tile_picked_phpair_abs_p_kernel(
         interleave_own(nc.vector.tensor_copy, 1, 1)
         quantise_w1(0, 1, 1)
         first_product(0, 1)
-        interleave_mixed(nc.vector.tensor_copy, 1, 1)
         quantise_w1(0, 2, 2)
         quantise_w1(1, 1, 1)
         first_product(1, 1)
+        interleave_mixed(nc.scalar.copy, 1, 1)
         quantise_w1(1, 2, 2)
 
-        evacuate(1, 0, BANK)
-        evacuate(1, BANK, S)
+        for s0, s1 in SPANS[1]:
+            evacuate(1, s0, s1)
         for t in (2, 3):
             for z in range(PASSES):
                 first_product(z, t)
         evacuate(2, 0, BANK)
-        evacuate(2, BANK, S - 64)
-        evacuate(3, 0, BANK)
-        evacuate(3, BANK, S)
-        evacuate(2, S - 64, S)
+        evacuate(2, BANK, S - LAST_COPY)
+        for s0, s1 in SPANS[3]:
+            evacuate(3, s0, s1)
+        evacuate(2, S - LAST_COPY, S)
 
-        diff = keep.tile([P, 4, V], F32, name="diff")
+        diff = keep.tile([P, 4, V], F32, name="diff", tag="word_table0", align_bytes=64)
         moving = keep.tile([P, V], F32, name="moving")
         lefts = []
         for t in range(4):
             lefts.append(keep.tile([P, V], F32, name="left%d" % t, tag="left%d" % t, align_bytes=64))
 
-        left_from = {}
-
-        def fetch_left(t, v0, v1):
-            left_from[t] = v0
-            nc.vector.tensor_copy(lefts[t][:, 0 : v1 - v0], h[t][:].indirect(left_sb[:, v0 // 16 : v1 // 16]))
+        def fetch_left(dst, t, v0, v1):
+            nc.vector.tensor_copy(dst, h[t][:].indirect(left_sb[:, v0 // LIST : v1 // LIST]))
 
         def subtract(dst, values, t, v0, v1):
-            nc.vector.tensor_tensor(
-                dst,
-                h[t][:].indirect(right_sb[:, v0 // 16 : v1 // 16]),
-                values,
-                SUB,
-            )
+            nc.vector.tensor_tensor(dst, h[t][:].indirect(right_sb[:, v0 // LIST : v1 // LIST]), values, SUB)
 
-        halves = ((0, V // 2), (V // 2, V))
-        for v0, v1 in halves:
-            nc.vector.tensor_copy(lefts[0][:, v0:v1], h[0][:].indirect(left_sb[:, v0 // 16 : v1 // 16]))
-        for v0, v1 in halves:
-            subtract(diff[:, 0, v0:v1], lefts[0][:, v0:v1], 0, v0, v1)
-        nc.sync.dma_start(diff[0:64, 1, :], diff[64:P, 0, :])
+        fetch_left(lefts[0][:, 0:V], 0, 0, V)
+        subtract(diff[:, 0, :], lefts[0][:], 0, 0, V)
+        nc.sync.dma_start(diff[0:LOW, 1, :], diff[LOW:P, 0, :])
 
         w2_raw = keep.tile([P, 4 * N], F32, name="w2_raw", tag="left0", align_bytes=64)
         w2_rows = w2.rearrange("(g t e) m -> t g e m", t=4, e=4)
@@ -224,28 +215,31 @@ def tile_picked_phpair_abs_p_kernel(
             nc.sync.dma_start(w2_raw[:, t * N : (t + 1) * N], w2_rows[t])
         w2_grouped = keep.tile([P, 4 * N], BF16, name="w2_grouped", align_bytes=64)
         nc.scalar.copy(
-            w2_grouped[:].rearrange("p (c i t) -> p c t i", i=4, t=4),
-            w2_raw[:].rearrange("p (t c i) -> p c t i", t=4, i=4),
+            w2_grouped[:].rearrange("p (c n t) -> p c t n", n=4, t=4),
+            w2_raw[:].rearrange("p (t c n) -> p c t n", t=4, n=4),
         )
 
+        halves = ((0, V // 2), (V // 2, V))
         for v0, v1 in halves:
-            nc.vector.tensor_copy(lefts[1][:, v0:v1], h[1][:].indirect(left_sb[:, v0 // 16 : v1 // 16]))
+            fetch_left(lefts[1][:, v0:v1], 1, v0, v1)
         for v0, v1 in halves:
             subtract(moving[:, v0:v1], lefts[1][:, v0:v1], 1, v0, v1)
-            nc.sync.dma_start(diff[64:P, 0, v0:v1], moving[0:64, v0:v1])
-            nc.sync.dma_start(diff[64:P, 1, v0:v1], moving[64:P, v0:v1])
+            nc.sync.dma_start(diff[LOW:P, 0, v0:v1], moving[0:LOW, v0:v1])
+            nc.sync.dma_start(diff[LOW:P, 1, v0:v1], moving[LOW:P, v0:v1])
 
         z_grouped = []
         for c, (v0, v1) in enumerate(CHUNKS):
-            if v0 % 128 == 0:
+            fetched = v0 - v0 % LEFT_MIN
+            if v0 == fetched:
+                upto = max(v1, v0 + LEFT_MIN)
                 for t in (3, 2):
-                    fetch_left(t, v0, max(v1, v0 + 128))
+                    fetch_left(lefts[t][:, 0 : upto - v0], t, v0, upto)
             for t in (3, 2):
-                subtract(diff[:, t, v0:v1], lefts[t][:, v0 - left_from[t] : v1 - left_from[t]], t, v0, v1)
+                subtract(diff[:, t, v0:v1], lefts[t][:, v0 - fetched : v1 - fetched], t, v0, v1)
             z_grouped.append(keep.tile([P, 4 * (v1 - v0)], BF16, name="z_grouped%d" % c, align_bytes=64))
             nc.scalar.activation(
-                z_grouped[c][:].rearrange("p (c i t) -> p c t i", i=4, t=4),
-                diff[:, :, v0:v1].rearrange("p t (c i) -> p c t i", i=4),
+                z_grouped[c][:].rearrange("p (c n t) -> p c t n", n=4, t=4),
+                diff[:, :, v0:v1].rearrange("p t (c n) -> p c t n", n=4),
                 ABS,
             )
 
@@ -253,25 +247,22 @@ def tile_picked_phpair_abs_p_kernel(
         z_codes = keep.tile([P, V], U32, name="z_codes", tag="left3", align_bytes=64)
         z_scales = keep.tile([P, V], U8, name="z_scales", align_bytes=64)
 
-        def second_product(c, acc):
-            v0, v1 = CHUNKS[c]
-            codes, scales = z_codes[:, v0:v1], z_scales[:, v0:v1]
-            nc.vector.quantize_mx(out=codes.bitcast(FP8X4), scales=scales, in_=z_grouped[c][:])
-            nc.tensor.matmul_mx(
-                out=acc,
-                lhsT=w2_codes[:].bitcast(FP8X4),
-                lhsT_scale=w2_scales[:],
-                rhs=codes[:].bitcast(FP8X4),
-                rhs_scale=scales[:],
-                start=True,
-                stop=True,
-            )
-
         for n, group in enumerate(STORES):
             g0, g1 = CHUNKS[group[0]][0], CHUNKS[group[-1]][1]
             acc = psum.tile([P, g1 - g0], F32, name="acc%d" % n, tag="bank%d" % (2 + n))
             for c in group:
-                second_product(c, acc[:, CHUNKS[c][0] - g0 : CHUNKS[c][1] - g0])
+                v0, v1 = CHUNKS[c]
+                codes = z_codes[:, v0:v1].bitcast(FP8X4)
+                nc.vector.quantize_mx(out=codes, scales=z_scales[:, v0:v1], in_=z_grouped[c][:])
+                nc.tensor.matmul_mx(
+                    out=acc[:, v0 - g0 : v1 - g0],
+                    lhsT=w2_codes[:].bitcast(FP8X4),
+                    lhsT_scale=w2_scales[:],
+                    rhs=codes,
+                    rhs_scale=z_scales[:, v0:v1],
+                    start=True,
+                    stop=True,
+                )
             result = keep.tile([P, g1 - g0], F32, name="result%d" % n)
             copy = nc.vector.tensor_copy if n == len(STORES) - 1 else nc.scalar.copy
             copy(result[:], acc[:])

@@ -21,8 +21,13 @@ PASSES = K // 512
 BANK = 512
 BANKS = 8
 HALF = H // 2
+PIECE_BYTES = 4 * HALF * 4
+LATE = PIECE_BYTES
+TABLE_BYTES = 4 * T
+LAST_PICK = 768
 LIST = 16
 SPANS = (((0, 256), (256, 512), (512, 768), (768, 1024)),) + 3 * (((0, 512), (512, 1024)),)
+GROUPS = (SPANS[0],) + 3 * (((0, 512), (512, LAST_PICK), (LAST_PICK, 1024)),)
 CHUNKS = ((0, 256), (256, 384), (384, 448), (448, 512))
 LEFT_MIN = 128
 STORES = ((0,), (1,), (2, 3))
@@ -35,6 +40,7 @@ def tile_picked_phpair_abs_p_kernel(
     nc = tc.nc
     with ExitStack() as ctx:
         keep = ctx.enter_context(tc.tile_pool(name="keep", bufs=1))
+        placed = ctx.enter_context(tc.tile_pool(name="placed", bufs=1))
         psum = ctx.enter_context(tc.psum_pool(name="psum", bufs=1))
 
         offs_sb = keep.tile([P, S // LIST], U16, name="offs_sb")
@@ -49,58 +55,61 @@ def tile_picked_phpair_abs_p_kernel(
         nc.sync.dma_start(left_sb[:], left)
         nc.sync.dma_start(right_sb[:], right)
 
-        scale_table = keep.tile([P, T], U8, name="scale_table", tag="after_scales", align_bytes=64)
+        scale_table = keep.tile([P, T], U8, name="scale_table", align_bytes=64)
         x_plane = keep.tile([P, S], U8, name="x_plane", align_bytes=64)
         nc.vector.memset(scale_table[:].bitcast(I32), 0)
-        nc.vector.memset(x_plane[:].bitcast(I32), 0)
         scale_rows = x_scales.rearrange("z (r e) c -> e r z c", e=2)
         for e in range(2):
             nc.sync.dma_start(scale_table[e:P:8, :].bitcast(I32), scale_rows[e].bitcast(I32))
 
-        word_table = []
-        for z in range(PASSES):
-            table = keep.tile([P, T], U32, name="word_table%d" % z, tag="word_table%d" % z, align_bytes=64)
-            nc.sync.dma_start(table[:].bitcast(I32), x_words[z].rearrange("p c r -> p (c r)").bitcast(I32))
-            word_table.append(table)
+        word_table = [
+            keep.tile([P, T], U32, name="word_table0", align_bytes=64),
+            keep.tile([P, T], U32, name="word_table1", align_bytes=64),
+        ]
+        word_rows = [x_words[z].rearrange("p c r -> p (c r)").bitcast(I32) for z in range(PASSES)]
+        for c0 in (0, T // 2):
+            nc.sync.dma_start(word_table[0][:, c0 : c0 + T // 2].bitcast(I32), word_rows[0][:, c0 : c0 + T // 2])
         nc.sync.dma_start(first_view[:, 2:4, :], first_rows[:, 2:4, :])
+        nc.sync.dma_start(word_table[1][:].bitcast(I32), word_rows[1])
 
         w1_raw = {(0, 0): w1_first}
 
-        def load_w1(z, hf, tag):
-            raw = keep.tile([P, 4 * HALF], F32, name="w1_raw%d%d" % (z, hf), tag=tag, align_bytes=64)
+        def load_w1(z, hf, raw):
             nc.sync.dma_start(
                 raw[:].rearrange("p (j c) -> p j c", j=4),
                 w1[512 * z : 512 * (z + 1), HALF * hf : HALF * (hf + 1)].rearrange("(p j) c -> p j c", j=4),
             )
             w1_raw[z, hf] = raw
 
-        load_w1(1, 0, "w1_next")
+        load_w1(1, 0, keep.tile([P, 4 * HALF], F32, name="w1_raw10", tag="w1_raw10", align_bytes=64))
 
-        picked_scales = keep.tile([P, S], U8, name="picked_scales", align_bytes=64)
+        picked_scales = placed.tile([P, S], U8, name="picked_scales", offset=PIECE_BYTES - S // 2, align_bytes=64)
         nc.vector.tensor_copy(picked_scales[:], scale_table[:].indirect(offs_sb[:]))
-        for e in range(2):
-            nc.sync.dma_start(x_plane[e:P:8, :].bitcast(I32), picked_scales[e:P:8, :].bitcast(I32))
+        nc.vector.tensor_copy(x_plane[:].bitcast(I32), picked_scales[:].bitcast(I32))
         for z in range(PASSES):
             for e in range(2):
                 nc.sync.dma_start(
                     x_plane[8 * z + 2 + e : P : 32, :].bitcast(I32),
-                    picked_scales[16 + 8 * z + e : P : 32, :].bitcast(I32),
+                    x_plane[16 + 8 * z + e : P : 32, :].bitcast(I32),
                 )
-        load_w1(0, 1, "after_scales")
+        load_w1(0, 1, placed.tile([P, 4 * HALF], F32, name="w1_raw01", offset=0, align_bytes=64))
+        load_w1(1, 1, placed.tile([P, 4 * HALF], F32, name="w1_raw11", offset=LATE, align_bytes=64))
 
         picked = {}
 
         def pick_words(z, s0, s1, tag):
             words = keep.tile([P, s1 - s0], U32, name="picked%d_%d" % (z, s0), tag=tag, align_bytes=64)
             nc.vector.tensor_copy(words[:], word_table[z][:].indirect(offs_sb[:, s0 // LIST : s1 // LIST]))
-            for n in range(s0 // BANK, s1 // BANK):
-                picked[z, n] = words[:, n * BANK - s0 : (n + 1) * BANK - s0]
+            picked[z, s0] = words
 
-        staging = keep.tile([P, 6 * P], BF16, name="staging", align_bytes=64)
-        grouped = {(1, 0): staging[:, 0 : 4 * P], (0, 1): staging[:, 2 * P : 6 * P]}
-        grouped[0, 0] = keep.tile([P, 4 * P], BF16, name="grouped00", tag="grouped00", align_bytes=64)
-        grouped[1, 1] = keep.tile([P, 4 * P], BF16, name="grouped11", tag="left0", align_bytes=64)
-        grouped[0, 2] = keep.tile([P, 8 * P], BF16, name="grouped02", align_bytes=64)
+        def picked_words(z, s0, s1):
+            start = max(a for y, a in picked if y == z and a <= s0)
+            return picked[z, start][:, s0 - start : s1 - start]
+
+        staging = keep.tile([P, 10 * P], BF16, name="staging", align_bytes=64)
+        grouped = {(0, 2): staging[:, 0 : 8 * P], (0, 1): staging[:, 6 * P : 10 * P]}
+        grouped[0, 0] = keep.tile([P, 4 * P], BF16, name="grouped00", align_bytes=64)
+        grouped[1, 0] = keep.tile([P, 4 * P], BF16, name="grouped10", align_bytes=64)
         grouped[1, 2] = keep.tile([P, 8 * P], BF16, name="grouped12", align_bytes=64)
 
         def plane_pair(z, hf, pair):
@@ -115,33 +124,45 @@ def tile_picked_phpair_abs_p_kernel(
                 plane_pair(z, hf, 1),
             )
 
-        def quantise(values, width, name):
-            codes = keep.tile([P, width], U32, name=name + "_codes", align_bytes=64)
-            scales = keep.tile([P, width], U8, name=name + "_scales", align_bytes=64)
+        def mx_tile(width, dtype, name, offset):
+            if offset is None:
+                return keep.tile([P, width], dtype, name=name, align_bytes=64)
+            return placed.tile([P, width], dtype, name=name, offset=offset, align_bytes=64)
+
+        def quantise(values, width, name, codes_at=None, scales_at=None):
+            codes = mx_tile(width, U32, name + "_codes", codes_at)
+            scales = mx_tile(width, U8, name + "_scales", scales_at)
             nc.vector.quantize_mx(out=codes[:].bitcast(FP8X4), scales=scales[:], in_=values[:])
             return codes, scales
 
         w1_mx = {}
+        end = LATE + TABLE_BYTES
+        places = {(0, 2): (end, None), (1, 2): (end + 8 * P, None)}
 
         def quantise_w1(z, t, tiles):
-            codes, scales = quantise(grouped[z, t], P * tiles, "w1_%d%d" % (z, t))
+            codes, scales = quantise(grouped[z, t], P * tiles, "w1_%d%d" % (z, t), *places.get((z, t), ()))
             for n in range(tiles):
                 w1_mx[z, t + n] = (codes[:, P * n : P * (n + 1)], scales[:, P * n : P * (n + 1)])
 
         banks = {}
-
-        def first_product(z, t):
-            codes, scales = w1_mx[z, t]
+        for t in range(4):
             dealt = sum(len(spans) for spans in SPANS[:t])
             for n, (s0, s1) in enumerate(SPANS[t]):
-                if z == 0:
-                    tag = "bank%d" % ((dealt + n) % BANKS)
-                    banks[t, s0] = psum.tile([P, s1 - s0], F32, name="bank%d_%d" % (t, s0), tag=tag)
+                tag = "bank%d" % ((dealt + n) % BANKS)
+                banks[t, s0] = psum.tile([P, s1 - s0], F32, name="bank%d_%d" % (t, s0), tag=tag)
+
+        def in_bank(t, s0, s1):
+            start = max(a for a, b in SPANS[t] if a <= s0)
+            return banks[t, start][:, s0 - start : s1 - start]
+
+        def first_product(z, t, groups):
+            codes, scales = w1_mx[z, t]
+            for s0, s1 in groups:
                 nc.tensor.matmul_mx(
-                    out=banks[t, s0][:],
+                    out=in_bank(t, s0, s1),
                     lhsT=codes.bitcast(FP8X4),
                     lhsT_scale=scales,
-                    rhs=picked[z, s0 // BANK][:, s0 % BANK : s0 % BANK + s1 - s0].bitcast(FP8X4),
+                    rhs=picked_words(z, s0, s1).bitcast(FP8X4),
                     rhs_scale=x_plane[8 * z : P, s0:s1],
                     start=(z == 0),
                     stop=(z == PASSES - 1),
@@ -150,54 +171,62 @@ def tile_picked_phpair_abs_p_kernel(
         h = {}
 
         def evacuate(t, s0, s1):
-            start = max(a for a, b in SPANS[t] if a <= s0)
-            nc.scalar.copy(h[t][:, s0:s1], banks[t, start][:, s0 - start : s1 - start])
+            nc.scalar.copy(h[t][:, s0:s1], in_bank(t, s0, s1))
 
         pick_words(0, 0, S, "picked0")
-        load_w1(1, 1, "word_table0")
-        pick_words(1, 0, BANK, "picked1")
         interleave_own(nc.scalar.copy, 0, 0)
         quantise_w1(0, 0, 1)
-        first_product(0, 0)
+        first_product(0, 0, GROUPS[0])
         interleave_mixed(nc.scalar.copy, 0, 0)
-        pick_words(1, BANK, S, "w1_first")
+        pick_words(1, 0, LAST_PICK, "picked1")
         interleave_own(nc.scalar.copy, 1, 0)
         quantise_w1(1, 0, 1)
-        first_product(1, 0)
-
         interleave_mixed(nc.scalar.copy, 1, 0)
-        interleave_own(nc.vector.tensor_copy, 0, 1)
-        interleave_mixed(nc.scalar.copy, 0, 1)
-        h[0] = keep.tile([P, S], F32, name="h0", tag="after_scales", align_bytes=64)
-        for t in range(1, 4):
+        pick_words(1, LAST_PICK, S, "w1_raw10")
+        first_product(1, 0, GROUPS[0])
+        for t in range(4):
             h[t] = keep.tile([P, S], F32, name="h%d" % t)
         for s0, s1 in SPANS[0]:
             evacuate(0, s0, s1)
-        interleave_own(nc.vector.tensor_copy, 1, 1)
+
+        interleave_own(nc.vector.tensor_copy, 0, 1)
         quantise_w1(0, 1, 1)
-        first_product(0, 1)
-        quantise_w1(0, 2, 2)
-        quantise_w1(1, 1, 1)
-        first_product(1, 1)
-        interleave_mixed(nc.scalar.copy, 1, 1)
-        quantise_w1(1, 2, 2)
+        last = []
+        for t, tag in enumerate(("left0", "last1")):
+            last.append(keep.tile([P, 4 * LOW], BF16, name="last%d" % t, tag=tag, align_bytes=64))
+            nc.vector.tensor_copy(last[t][:].rearrange("p (g e j) -> p g j e", e=4, j=4), plane_pair(1, 1, 0)[:, t])
+        codes = mx_tile(P, U32, "w1_11_codes", end - 2 * P)
+        scales = mx_tile(P, U8, "w1_11_scales", end + 8 * P)
+        for t in range(2):
+            columns = slice(LOW * t, LOW * (t + 1))
+            nc.vector.quantize_mx(out=codes[:, columns].bitcast(FP8X4), scales=scales[:, columns], in_=last[t][:])
+        w1_mx[1, 1] = (codes[:], scales[:])
+        for groups in (GROUPS[1][:2], GROUPS[1][2:]):
+            for z in range(PASSES):
+                first_product(z, 1, groups)
+        for z in range(PASSES):
+            interleave_mixed(nc.scalar.copy, z, 1)
+            quantise_w1(z, 2, 2)
 
         for s0, s1 in SPANS[1]:
             evacuate(1, s0, s1)
         for t in (2, 3):
             for z in range(PASSES):
-                first_product(z, t)
+                first_product(z, t, GROUPS[t][:1])
+        for t in (2, 3):
+            for group in GROUPS[t][1:]:
+                for z in range(PASSES):
+                    first_product(z, t, (group,))
         evacuate(2, 0, BANK)
+        evacuate(3, 0, BANK)
         evacuate(2, BANK, S - LAST_COPY)
-        for s0, s1 in SPANS[3]:
-            evacuate(3, s0, s1)
+        evacuate(3, BANK, S)
         evacuate(2, S - LAST_COPY, S)
 
-        diff = keep.tile([P, 4, V], F32, name="diff", tag="word_table0", align_bytes=64)
+        diff = placed.tile([P, 4, V], F32, name="diff", offset=LATE, align_bytes=64)
         moving = keep.tile([P, V], F32, name="moving")
-        lefts = []
-        for t in range(4):
-            lefts.append(keep.tile([P, V], F32, name="left%d" % t, tag="left%d" % t, align_bytes=64))
+        lefts = {0: keep.tile([P, V], F32, name="left0", tag="left0", align_bytes=64)}
+        rings = [keep.tile([P, V // 2], F32, name="ring%d" % n, tag="ring%d" % n, align_bytes=64) for n in range(2)]
 
         def fetch_left(dst, t, v0, v1):
             nc.vector.tensor_copy(dst, h[t][:].indirect(left_sb[:, v0 // LIST : v1 // LIST]))
@@ -220,22 +249,24 @@ def tile_picked_phpair_abs_p_kernel(
         )
 
         halves = ((0, V // 2), (V // 2, V))
-        for v0, v1 in halves:
-            fetch_left(lefts[1][:, v0:v1], 1, v0, v1)
-        for v0, v1 in halves:
-            subtract(moving[:, v0:v1], lefts[1][:, v0:v1], 1, v0, v1)
+        for (v0, v1), ring in zip(halves, rings):
+            fetch_left(ring[:], 1, v0, v1)
+        for (v0, v1), ring in zip(halves, rings):
+            subtract(moving[:, v0:v1], ring[:], 1, v0, v1)
             nc.sync.dma_start(diff[LOW:P, 0, v0:v1], moving[0:LOW, v0:v1])
             nc.sync.dma_start(diff[LOW:P, 1, v0:v1], moving[LOW:P, v0:v1])
 
         z_grouped = []
+        order = (2, 3)
         for c, (v0, v1) in enumerate(CHUNKS):
             fetched = v0 - v0 % LEFT_MIN
             if v0 == fetched:
                 upto = max(v1, v0 + LEFT_MIN)
-                for t in (3, 2):
-                    fetch_left(lefts[t][:, 0 : upto - v0], t, v0, upto)
-            for t in (3, 2):
-                subtract(diff[:, t, v0:v1], lefts[t][:, v0 - fetched : v1 - fetched], t, v0, v1)
+                order = order[::-1]
+                for t, ring in zip(order, rings):
+                    fetch_left(ring[:, 0 : upto - v0], t, v0, upto)
+            for t, ring in zip(order, rings):
+                subtract(diff[:, t, v0:v1], ring[:, v0 - fetched : v1 - fetched], t, v0, v1)
             z_grouped.append(keep.tile([P, 4 * (v1 - v0)], BF16, name="z_grouped%d" % c, align_bytes=64))
             nc.scalar.activation(
                 z_grouped[c][:].rearrange("p (c n t) -> p c t n", n=4, t=4),
@@ -244,7 +275,7 @@ def tile_picked_phpair_abs_p_kernel(
             )
 
         w2_codes, w2_scales = quantise(w2_grouped, N, "w2")
-        z_codes = keep.tile([P, V], U32, name="z_codes", tag="left3", align_bytes=64)
+        z_codes = keep.tile([P, V], U32, name="z_codes", tag="ring0", align_bytes=64)
         z_scales = keep.tile([P, V], U8, name="z_scales", align_bytes=64)
 
         for n, group in enumerate(STORES):

@@ -24,12 +24,10 @@ HALF = H // 2
 PIECE_BYTES = 4 * HALF * 4
 LATE = PIECE_BYTES
 TABLE_BYTES = 4 * T
-LAST_PICK = 768
 LIST = 16
 SPANS = (((0, 256), (256, 512), (512, 768), (768, 1024)),) + 3 * (((0, 512), (512, 1024)),)
-GROUPS = (SPANS[0],) + 3 * (((0, 512), (512, LAST_PICK), (LAST_PICK, 1024)),)
 CHUNKS = ((0, 256), (256, 384), (384, 448), (448, 512))
-LEFT_MIN = 128
+LEFTS = ((0, 256), (256, 384), (384, 512))
 STORES = ((0,), (1,), (2, 3))
 LAST_COPY = 64
 
@@ -55,9 +53,10 @@ def tile_picked_phpair_abs_p_kernel(
         nc.sync.dma_start(left_sb[:], left)
         nc.sync.dma_start(right_sb[:], right)
 
-        scale_table = keep.tile([P, T], U8, name="scale_table", align_bytes=64)
+        scale_table = placed.tile([P, T], U8, name="scale_table", offset=PIECE_BYTES - T // 2, align_bytes=64)
         x_plane = keep.tile([P, S], U8, name="x_plane", align_bytes=64)
         nc.vector.memset(scale_table[:].bitcast(I32), 0)
+        nc.vector.memset(x_plane[:].bitcast(I32), 0)
         scale_rows = x_scales.rearrange("z (r e) c -> e r z c", e=2)
         for e in range(2):
             nc.sync.dma_start(scale_table[e:P:8, :].bitcast(I32), scale_rows[e].bitcast(I32))
@@ -81,16 +80,17 @@ def tile_picked_phpair_abs_p_kernel(
             )
             w1_raw[z, hf] = raw
 
-        load_w1(1, 0, keep.tile([P, 4 * HALF], F32, name="w1_raw10", tag="w1_raw10", align_bytes=64))
+        load_w1(1, 0, keep.tile([P, 4 * HALF], F32, name="w1_raw10", align_bytes=64))
 
-        picked_scales = placed.tile([P, S], U8, name="picked_scales", offset=PIECE_BYTES - S // 2, align_bytes=64)
+        picked_scales = keep.tile([P, S], U8, name="picked_scales", align_bytes=64)
         nc.vector.tensor_copy(picked_scales[:], scale_table[:].indirect(offs_sb[:]))
-        nc.vector.tensor_copy(x_plane[:].bitcast(I32), picked_scales[:].bitcast(I32))
+        for e in range(2):
+            nc.sync.dma_start(x_plane[e:P:8, :].bitcast(I32), picked_scales[e:P:8, :].bitcast(I32))
         for z in range(PASSES):
             for e in range(2):
                 nc.sync.dma_start(
                     x_plane[8 * z + 2 + e : P : 32, :].bitcast(I32),
-                    x_plane[16 + 8 * z + e : P : 32, :].bitcast(I32),
+                    picked_scales[16 + 8 * z + e : P : 32, :].bitcast(I32),
                 )
         load_w1(0, 1, placed.tile([P, 4 * HALF], F32, name="w1_raw01", offset=0, align_bytes=64))
         load_w1(1, 1, placed.tile([P, 4 * HALF], F32, name="w1_raw11", offset=LATE, align_bytes=64))
@@ -106,11 +106,9 @@ def tile_picked_phpair_abs_p_kernel(
             start = max(a for y, a in picked if y == z and a <= s0)
             return picked[z, start][:, s0 - start : s1 - start]
 
-        staging = keep.tile([P, 10 * P], BF16, name="staging", align_bytes=64)
-        grouped = {(0, 2): staging[:, 0 : 8 * P], (0, 1): staging[:, 6 * P : 10 * P]}
-        grouped[0, 0] = keep.tile([P, 4 * P], BF16, name="grouped00", align_bytes=64)
-        grouped[1, 0] = keep.tile([P, 4 * P], BF16, name="grouped10", align_bytes=64)
-        grouped[1, 2] = keep.tile([P, 8 * P], BF16, name="grouped12", align_bytes=64)
+        grouped = {}
+        for z, t, tiles in ((0, 0, 1), (1, 0, 1), (0, 1, 1), (0, 2, 2), (1, 2, 2)):
+            grouped[z, t] = keep.tile([P, 4 * P * tiles], BF16, name="grouped%d%d" % (z, t), align_bytes=64)
 
         def plane_pair(z, hf, pair):
             return w1_raw[z, hf][:].rearrange("p (j g s t e) -> p s t g j e", j=4, s=2, t=2, e=4)[:, pair]
@@ -137,7 +135,7 @@ def tile_picked_phpair_abs_p_kernel(
 
         w1_mx = {}
         end = LATE + TABLE_BYTES
-        places = {(0, 2): (end, None), (1, 2): (end + 8 * P, None)}
+        places = {(1, 2): (end, None)}
 
         def quantise_w1(z, t, tiles):
             codes, scales = quantise(grouped[z, t], P * tiles, "w1_%d%d" % (z, t), *places.get((z, t), ()))
@@ -176,47 +174,48 @@ def tile_picked_phpair_abs_p_kernel(
         pick_words(0, 0, S, "picked0")
         interleave_own(nc.scalar.copy, 0, 0)
         quantise_w1(0, 0, 1)
-        first_product(0, 0, GROUPS[0])
+        first_product(0, 0, SPANS[0])
         interleave_mixed(nc.scalar.copy, 0, 0)
-        pick_words(1, 0, LAST_PICK, "picked1")
+        pick_words(1, 0, S, "picked1")
         interleave_own(nc.scalar.copy, 1, 0)
         quantise_w1(1, 0, 1)
         interleave_mixed(nc.scalar.copy, 1, 0)
-        pick_words(1, LAST_PICK, S, "w1_raw10")
-        first_product(1, 0, GROUPS[0])
+        first_product(1, 0, SPANS[0])
         for t in range(4):
             h[t] = keep.tile([P, S], F32, name="h%d" % t)
         for s0, s1 in SPANS[0]:
             evacuate(0, s0, s1)
 
         interleave_own(nc.vector.tensor_copy, 0, 1)
+        interleave_mixed(nc.vector.tensor_copy, 0, 1)
         quantise_w1(0, 1, 1)
+        shared_scales = keep.tile([P, 2 * P], U8, name="shared_scales", align_bytes=64)
+        codes = mx_tile(2 * P, U32, "w1_02_codes", None)
+        nc.vector.quantize_mx(out=codes[:].bitcast(FP8X4), scales=shared_scales[4:P, :], in_=grouped[0, 2][:])
+        for n in range(2):
+            w1_mx[0, 2 + n] = (codes[:, P * n : P * (n + 1)], shared_scales[4:P, P * n : P * (n + 1)])
+        first_product(0, 1, SPANS[1])
         last = []
         for t, tag in enumerate(("left0", "last1")):
             last.append(keep.tile([P, 4 * LOW], BF16, name="last%d" % t, tag=tag, align_bytes=64))
             nc.vector.tensor_copy(last[t][:].rearrange("p (g e j) -> p g j e", e=4, j=4), plane_pair(1, 1, 0)[:, t])
         codes = mx_tile(P, U32, "w1_11_codes", end - 2 * P)
-        scales = mx_tile(P, U8, "w1_11_scales", end + 8 * P)
+        scales = shared_scales[:, LOW : LOW + P]
         for t in range(2):
             columns = slice(LOW * t, LOW * (t + 1))
             nc.vector.quantize_mx(out=codes[:, columns].bitcast(FP8X4), scales=scales[:, columns], in_=last[t][:])
-        w1_mx[1, 1] = (codes[:], scales[:])
-        for groups in (GROUPS[1][:2], GROUPS[1][2:]):
-            for z in range(PASSES):
-                first_product(z, 1, groups)
-        for z in range(PASSES):
-            interleave_mixed(nc.scalar.copy, z, 1)
-            quantise_w1(z, 2, 2)
+        w1_mx[1, 1] = (codes[:], scales)
+        first_product(1, 1, SPANS[1])
+        for t in (2, 3):
+            first_product(0, t, SPANS[t])
+        interleave_mixed(nc.scalar.copy, 1, 1)
+        quantise_w1(1, 2, 2)
 
         for s0, s1 in SPANS[1]:
             evacuate(1, s0, s1)
-        for t in (2, 3):
-            for z in range(PASSES):
-                first_product(z, t, GROUPS[t][:1])
-        for t in (2, 3):
-            for group in GROUPS[t][1:]:
-                for z in range(PASSES):
-                    first_product(z, t, (group,))
+        for bank in range(2):
+            for t in (2, 3):
+                first_product(1, t, SPANS[t][bank : bank + 1])
         evacuate(2, 0, BANK)
         evacuate(3, 0, BANK)
         evacuate(2, BANK, S - LAST_COPY)
@@ -226,7 +225,7 @@ def tile_picked_phpair_abs_p_kernel(
         diff = placed.tile([P, 4, V], F32, name="diff", offset=LATE, align_bytes=64)
         moving = keep.tile([P, V], F32, name="moving")
         lefts = {0: keep.tile([P, V], F32, name="left0", tag="left0", align_bytes=64)}
-        rings = [keep.tile([P, V // 2], F32, name="ring%d" % n, tag="ring%d" % n, align_bytes=64) for n in range(2)]
+        rings = [keep.tile([P, LEFTS[0][1]], F32, name="ring%d" % n, tag="ring%d" % n, align_bytes=64) for n in range(2)]
 
         def fetch_left(dst, t, v0, v1):
             nc.vector.tensor_copy(dst, h[t][:].indirect(left_sb[:, v0 // LIST : v1 // LIST]))
@@ -250,18 +249,17 @@ def tile_picked_phpair_abs_p_kernel(
 
         halves = ((0, V // 2), (V // 2, V))
         for (v0, v1), ring in zip(halves, rings):
-            fetch_left(ring[:], 1, v0, v1)
+            fetch_left(ring[:, 0 : v1 - v0], 1, v0, v1)
         for (v0, v1), ring in zip(halves, rings):
-            subtract(moving[:, v0:v1], ring[:], 1, v0, v1)
+            subtract(moving[:, v0:v1], ring[:, 0 : v1 - v0], 1, v0, v1)
             nc.sync.dma_start(diff[LOW:P, 0, v0:v1], moving[0:LOW, v0:v1])
             nc.sync.dma_start(diff[LOW:P, 1, v0:v1], moving[LOW:P, v0:v1])
 
         z_grouped = []
         order = (2, 3)
         for c, (v0, v1) in enumerate(CHUNKS):
-            fetched = v0 - v0 % LEFT_MIN
+            fetched, upto = [stretch for stretch in LEFTS if stretch[0] <= v0][-1]
             if v0 == fetched:
-                upto = max(v1, v0 + LEFT_MIN)
                 order = order[::-1]
                 for t, ring in zip(order, rings):
                     fetch_left(ring[:, 0 : upto - v0], t, v0, upto)

@@ -22,13 +22,15 @@ BANK = 512
 BANKS = 8
 HALF = H // 2
 PIECE_BYTES = 4 * HALF * 4
-LATE = PIECE_BYTES
+LATE = 2 * PIECE_BYTES
 TABLE_BYTES = 4 * T
 LIST = 16
-SPANS = (((0, 256), (256, 512), (512, 768), (768, 1024)),) + 3 * (((0, 512), (512, 1024)),)
+SPANS = 2 * (((0, 256), (256, 512), (512, 768), (768, 1024)),) + 2 * (((0, 512), (512, 1024)),)
 CHUNKS = ((0, 256), (256, 384), (384, 448), (448, 512))
 LEFTS = ((0, 256), (256, 384), (384, 512))
 STORES = ((0,), (1,), (2, 3))
+FIRST = 384
+CUT = 768
 LAST_COPY = 64
 
 
@@ -53,7 +55,7 @@ def tile_picked_phpair_abs_p_kernel(
         nc.sync.dma_start(left_sb[:], left)
         nc.sync.dma_start(right_sb[:], right)
 
-        scale_table = placed.tile([P, T], U8, name="scale_table", offset=PIECE_BYTES - T // 2, align_bytes=64)
+        scale_table = placed.tile([P, T], U8, name="scale_table", offset=LATE - T // 2, align_bytes=64)
         x_plane = keep.tile([P, S], U8, name="x_plane", align_bytes=64)
         nc.vector.memset(scale_table[:].bitcast(I32), 0)
         nc.vector.memset(x_plane[:].bitcast(I32), 0)
@@ -80,9 +82,10 @@ def tile_picked_phpair_abs_p_kernel(
             )
             w1_raw[z, hf] = raw
 
+
         load_w1(1, 0, keep.tile([P, 4 * HALF], F32, name="w1_raw10", align_bytes=64))
 
-        picked_scales = keep.tile([P, S], U8, name="picked_scales", align_bytes=64)
+        picked_scales = keep.tile([P, S], U8, name="picked_scales", tag="picked_scales", align_bytes=64)
         nc.vector.tensor_copy(picked_scales[:], scale_table[:].indirect(offs_sb[:]))
         for e in range(2):
             nc.sync.dma_start(x_plane[e:P:8, :].bitcast(I32), picked_scales[e:P:8, :].bitcast(I32))
@@ -92,7 +95,7 @@ def tile_picked_phpair_abs_p_kernel(
                     x_plane[8 * z + 2 + e : P : 32, :].bitcast(I32),
                     picked_scales[16 + 8 * z + e : P : 32, :].bitcast(I32),
                 )
-        load_w1(0, 1, placed.tile([P, 4 * HALF], F32, name="w1_raw01", offset=0, align_bytes=64))
+        load_w1(0, 1, placed.tile([P, 4 * HALF], F32, name="w1_raw01", offset=LATE - PIECE_BYTES, align_bytes=64))
         load_w1(1, 1, placed.tile([P, 4 * HALF], F32, name="w1_raw11", offset=LATE, align_bytes=64))
 
         picked = {}
@@ -107,8 +110,13 @@ def tile_picked_phpair_abs_p_kernel(
             return picked[z, start][:, s0 - start : s1 - start]
 
         grouped = {}
+
+        def stage(z, t, tiles):
+            tag = "left0" if (z, t) == (0, 2) else "grouped%d%d" % (z, t)
+            grouped[z, t] = keep.tile([P, 4 * P * tiles], BF16, name="grouped%d%d" % (z, t), tag=tag, align_bytes=64)
+
         for z, t, tiles in ((0, 0, 1), (1, 0, 1), (0, 1, 1), (0, 2, 2), (1, 2, 2)):
-            grouped[z, t] = keep.tile([P, 4 * P * tiles], BF16, name="grouped%d%d" % (z, t), align_bytes=64)
+            stage(z, t, tiles)
 
         def plane_pair(z, hf, pair):
             return w1_raw[z, hf][:].rearrange("p (j g s t e) -> p s t g j e", j=4, s=2, t=2, e=4)[:, pair]
@@ -124,7 +132,8 @@ def tile_picked_phpair_abs_p_kernel(
 
         def mx_tile(width, dtype, name, offset):
             if offset is None:
-                return keep.tile([P, width], dtype, name=name, align_bytes=64)
+                tag = {"w1_10_codes": "grouped11"}.get(name, name)
+                return keep.tile([P, width], dtype, name=name, tag=tag, align_bytes=64)
             return placed.tile([P, width], dtype, name=name, offset=offset, align_bytes=64)
 
         def quantise(values, width, name, codes_at=None, scales_at=None):
@@ -135,7 +144,7 @@ def tile_picked_phpair_abs_p_kernel(
 
         w1_mx = {}
         end = LATE + TABLE_BYTES
-        places = {(1, 2): (end, None)}
+        places = {}
 
         def quantise_w1(z, t, tiles):
             codes, scales = quantise(grouped[z, t], P * tiles, "w1_%d%d" % (z, t), *places.get((z, t), ()))
@@ -143,18 +152,25 @@ def tile_picked_phpair_abs_p_kernel(
                 w1_mx[z, t + n] = (codes[:, P * n : P * (n + 1)], scales[:, P * n : P * (n + 1)])
 
         banks = {}
+        tags = {}
         for t in range(4):
             dealt = sum(len(spans) for spans in SPANS[:t])
             for n, (s0, s1) in enumerate(SPANS[t]):
                 tag = "bank%d" % ((dealt + n) % BANKS)
-                banks[t, s0] = psum.tile([P, s1 - s0], F32, name="bank%d_%d" % (t, s0), tag=tag)
+                tags[t, s0] = (tag, s1 - s0)
 
         def in_bank(t, s0, s1):
             start = max(a for a, b in SPANS[t] if a <= s0)
+            if (t, start) not in banks:
+                tag, width = tags[t, start]
+                banks[t, start] = psum.tile([P, width], F32, name="bank%d_%d" % (t, start), tag=tag)
             return banks[t, start][:, s0 - start : s1 - start]
 
         def first_product(z, t, groups):
             codes, scales = w1_mx[z, t]
+            ends = [s1 for s0, s1 in groups]
+            if z == PASSES - 1:
+                groups = [part for a, b in groups for part in (((a, CUT), (CUT, b)) if a < CUT < b else ((a, b),))]
             for s0, s1 in groups:
                 nc.tensor.matmul_mx(
                     out=in_bank(t, s0, s1),
@@ -163,7 +179,7 @@ def tile_picked_phpair_abs_p_kernel(
                     rhs=picked_words(z, s0, s1).bitcast(FP8X4),
                     rhs_scale=x_plane[8 * z : P, s0:s1],
                     start=(z == 0),
-                    stop=(z == PASSES - 1),
+                    stop=(z == PASSES - 1 and s1 in ends),
                 )
 
         h = {}
@@ -172,42 +188,43 @@ def tile_picked_phpair_abs_p_kernel(
             nc.scalar.copy(h[t][:, s0:s1], in_bank(t, s0, s1))
 
         pick_words(0, 0, S, "picked0")
+        idle = psum.tile([P, BANK], F32, name="idle", tag="bank7")
+        for n in range(2):
+            nc.tensor.matmul_mx(
+                out=idle[:],
+                lhsT=picked_words(0, 0, P).bitcast(FP8X4),
+                lhsT_scale=picked_scales[:, 0:P],
+                rhs=picked_words(0, 0, BANK).bitcast(FP8X4),
+                rhs_scale=picked_scales[:, 0:BANK],
+                start=True,
+                stop=True,
+            )
         interleave_own(nc.scalar.copy, 0, 0)
         quantise_w1(0, 0, 1)
-        first_product(0, 0, SPANS[0])
         interleave_mixed(nc.scalar.copy, 0, 0)
-        pick_words(1, 0, S, "picked1")
+        pick_words(1, 0, CUT, "picked1")
         interleave_own(nc.scalar.copy, 1, 0)
         quantise_w1(1, 0, 1)
+        pick_words(1, CUT, S, "picked_scales")
         interleave_mixed(nc.scalar.copy, 1, 0)
-        first_product(1, 0, SPANS[0])
+        for span in SPANS[0]:
+            for z in range(PASSES):
+                first_product(z, 0, [span])
         for t in range(4):
             h[t] = keep.tile([P, S], F32, name="h%d" % t)
         for s0, s1 in SPANS[0]:
             evacuate(0, s0, s1)
 
-        interleave_own(nc.vector.tensor_copy, 0, 1)
         interleave_mixed(nc.vector.tensor_copy, 0, 1)
+        interleave_own(nc.vector.tensor_copy, 0, 1)
+        quantise_w1(0, 2, 2)
         quantise_w1(0, 1, 1)
-        shared_scales = keep.tile([P, 2 * P], U8, name="shared_scales", align_bytes=64)
-        codes = mx_tile(2 * P, U32, "w1_02_codes", None)
-        nc.vector.quantize_mx(out=codes[:].bitcast(FP8X4), scales=shared_scales[4:P, :], in_=grouped[0, 2][:])
-        for n in range(2):
-            w1_mx[0, 2 + n] = (codes[:, P * n : P * (n + 1)], shared_scales[4:P, P * n : P * (n + 1)])
-        first_product(0, 1, SPANS[1])
-        last = []
-        for t, tag in enumerate(("left0", "last1")):
-            last.append(keep.tile([P, 4 * LOW], BF16, name="last%d" % t, tag=tag, align_bytes=64))
-            nc.vector.tensor_copy(last[t][:].rearrange("p (g e j) -> p g j e", e=4, j=4), plane_pair(1, 1, 0)[:, t])
-        codes = mx_tile(P, U32, "w1_11_codes", end - 2 * P)
-        scales = shared_scales[:, LOW : LOW + P]
-        for t in range(2):
-            columns = slice(LOW * t, LOW * (t + 1))
-            nc.vector.quantize_mx(out=codes[:, columns].bitcast(FP8X4), scales=scales[:, columns], in_=last[t][:])
-        w1_mx[1, 1] = (codes[:], scales)
-        first_product(1, 1, SPANS[1])
-        for t in (2, 3):
+        for t in (1, 2, 3):
             first_product(0, t, SPANS[t])
+        stage(1, 1, 1)
+        interleave_own(nc.scalar.copy, 1, 1)
+        quantise_w1(1, 1, 1)
+        first_product(1, 1, SPANS[1])
         interleave_mixed(nc.scalar.copy, 1, 1)
         quantise_w1(1, 2, 2)
 
@@ -222,7 +239,7 @@ def tile_picked_phpair_abs_p_kernel(
         evacuate(3, BANK, S)
         evacuate(2, S - LAST_COPY, S)
 
-        diff = placed.tile([P, 4, V], F32, name="diff", offset=LATE, align_bytes=64)
+        diff = placed.tile([P, 4, V], F32, name="diff", offset=LATE + 1024, align_bytes=64)
         moving = keep.tile([P, V], F32, name="moving")
         lefts = {0: keep.tile([P, V], F32, name="left0", tag="left0", align_bytes=64)}
         rings = [keep.tile([P, LEFTS[0][1]], F32, name="ring%d" % n, tag="ring%d" % n, align_bytes=64) for n in range(2)]
@@ -233,8 +250,11 @@ def tile_picked_phpair_abs_p_kernel(
         def subtract(dst, values, t, v0, v1):
             nc.vector.tensor_tensor(dst, h[t][:].indirect(right_sb[:, v0 // LIST : v1 // LIST]), values, SUB)
 
-        fetch_left(lefts[0][:, 0:V], 0, 0, V)
-        subtract(diff[:, 0, :], lefts[0][:], 0, 0, V)
+        rest = placed.tile([P, V - FIRST], F32, name="left_rest", offset=LATE, align_bytes=64)
+        fetch_left(lefts[0][:, 0:FIRST], 0, 0, FIRST)
+        fetch_left(rest[:], 0, FIRST, V)
+        subtract(diff[:, 0, 0:FIRST], lefts[0][:, 0:FIRST], 0, 0, FIRST)
+        subtract(diff[:, 0, FIRST:V], rest[:], 0, FIRST, V)
         nc.sync.dma_start(diff[0:LOW, 1, :], diff[LOW:P, 0, :])
 
         w2_raw = keep.tile([P, 4 * N], F32, name="w2_raw", tag="left0", align_bytes=64)

@@ -22,15 +22,16 @@ BANK = 512
 BANKS = 8
 HALF = H // 2
 PIECE_BYTES = 4 * HALF * 4
-LATE = 2 * PIECE_BYTES
-TABLE_BYTES = 4 * T
+LAST_PIECE = 2 * PIECE_BYTES
 LIST = 16
-SPANS = 2 * (((0, 256), (256, 512), (512, 768), (768, 1024)),) + 2 * (((0, 512), (512, 1024)),)
-CHUNKS = ((0, 256), (256, 384), (384, 448), (448, 512))
-LEFTS = ((0, 256), (256, 384), (384, 512))
+QUARTERS = ((0, 256), (256, 512), (512, 768), (768, 1024))
+HALVES = ((0, 512), (512, 1024))
+SPANS = (QUARTERS, QUARTERS, HALVES, HALVES)
+WORD_CUT = 768
+LEFT_CUT = 384
+STRETCHES = ((0, 256), (256, 384), (384, 448), (448, 512))
+LEFTS = ((0, 384), (384, 512))
 STORES = ((0,), (1,), (2, 3))
-FIRST = 384
-CUT = 768
 LAST_COPY = 64
 
 
@@ -55,7 +56,7 @@ def tile_picked_phpair_abs_p_kernel(
         nc.sync.dma_start(left_sb[:], left)
         nc.sync.dma_start(right_sb[:], right)
 
-        scale_table = placed.tile([P, T], U8, name="scale_table", offset=LATE - T // 2, align_bytes=64)
+        scale_table = placed.tile([P, T], U8, name="scale_table", offset=LAST_PIECE - T // 2, align_bytes=64)
         x_plane = keep.tile([P, S], U8, name="x_plane", align_bytes=64)
         nc.vector.memset(scale_table[:].bitcast(I32), 0)
         nc.vector.memset(x_plane[:].bitcast(I32), 0)
@@ -82,7 +83,6 @@ def tile_picked_phpair_abs_p_kernel(
             )
             w1_raw[z, hf] = raw
 
-
         load_w1(1, 0, keep.tile([P, 4 * HALF], F32, name="w1_raw10", align_bytes=64))
 
         picked_scales = keep.tile([P, S], U8, name="picked_scales", tag="picked_scales", align_bytes=64)
@@ -95,8 +95,9 @@ def tile_picked_phpair_abs_p_kernel(
                     x_plane[8 * z + 2 + e : P : 32, :].bitcast(I32),
                     picked_scales[16 + 8 * z + e : P : 32, :].bitcast(I32),
                 )
-        load_w1(0, 1, placed.tile([P, 4 * HALF], F32, name="w1_raw01", offset=LATE - PIECE_BYTES, align_bytes=64))
-        load_w1(1, 1, placed.tile([P, 4 * HALF], F32, name="w1_raw11", offset=LATE, align_bytes=64))
+        third = LAST_PIECE - PIECE_BYTES
+        load_w1(0, 1, placed.tile([P, 4 * HALF], F32, name="w1_raw01", offset=third, align_bytes=64))
+        load_w1(1, 1, placed.tile([P, 4 * HALF], F32, name="w1_raw11", offset=LAST_PIECE, align_bytes=64))
 
         picked = {}
 
@@ -111,12 +112,14 @@ def tile_picked_phpair_abs_p_kernel(
 
         grouped = {}
 
-        def stage(z, t, tiles):
-            tag = "left0" if (z, t) == (0, 2) else "grouped%d%d" % (z, t)
+        def stage(z, t, tiles, tag):
             grouped[z, t] = keep.tile([P, 4 * P * tiles], BF16, name="grouped%d%d" % (z, t), tag=tag, align_bytes=64)
 
-        for z, t, tiles in ((0, 0, 1), (1, 0, 1), (0, 1, 1), (0, 2, 2), (1, 2, 2)):
-            stage(z, t, tiles)
+        stage(0, 0, 1, "grouped00")
+        stage(1, 0, 1, "grouped10")
+        stage(0, 1, 1, "grouped01")
+        stage(0, 2, 2, "left0")
+        stage(1, 2, 2, "grouped12")
 
         def plane_pair(z, hf, pair):
             return w1_raw[z, hf][:].rearrange("p (j g s t e) -> p s t g j e", j=4, s=2, t=2, e=4)[:, pair]
@@ -130,57 +133,44 @@ def tile_picked_phpair_abs_p_kernel(
                 plane_pair(z, hf, 1),
             )
 
-        def mx_tile(width, dtype, name, offset):
-            if offset is None:
-                tag = {"w1_10_codes": "grouped11"}.get(name, name)
-                return keep.tile([P, width], dtype, name=name, tag=tag, align_bytes=64)
-            return placed.tile([P, width], dtype, name=name, offset=offset, align_bytes=64)
-
-        def quantise(values, width, name, codes_at=None, scales_at=None):
-            codes = mx_tile(width, U32, name + "_codes", codes_at)
-            scales = mx_tile(width, U8, name + "_scales", scales_at)
+        def quantise(values, width, name):
+            codes = keep.tile([P, width], U32, name=name + "_codes", tag=name + "_codes", align_bytes=64)
+            scales = keep.tile([P, width], U8, name=name + "_scales", tag=name + "_scales", align_bytes=64)
             nc.vector.quantize_mx(out=codes[:].bitcast(FP8X4), scales=scales[:], in_=values[:])
             return codes, scales
 
         w1_mx = {}
-        end = LATE + TABLE_BYTES
-        places = {}
 
         def quantise_w1(z, t, tiles):
-            codes, scales = quantise(grouped[z, t], P * tiles, "w1_%d%d" % (z, t), *places.get((z, t), ()))
+            codes, scales = quantise(grouped[z, t], P * tiles, "w1_%d%d" % (z, t))
             for n in range(tiles):
                 w1_mx[z, t + n] = (codes[:, P * n : P * (n + 1)], scales[:, P * n : P * (n + 1)])
 
         banks = {}
-        tags = {}
-        for t in range(4):
-            dealt = sum(len(spans) for spans in SPANS[:t])
-            for n, (s0, s1) in enumerate(SPANS[t]):
-                tag = "bank%d" % ((dealt + n) % BANKS)
-                tags[t, s0] = (tag, s1 - s0)
 
         def in_bank(t, s0, s1):
-            start = max(a for a, b in SPANS[t] if a <= s0)
+            n = max(n for n, (a, b) in enumerate(SPANS[t]) if a <= s0)
+            start, end = SPANS[t][n]
             if (t, start) not in banks:
-                tag, width = tags[t, start]
-                banks[t, start] = psum.tile([P, width], F32, name="bank%d_%d" % (t, start), tag=tag)
+                tag = "bank%d" % ((sum(len(spans) for spans in SPANS[:t]) + n) % BANKS)
+                banks[t, start] = psum.tile([P, end - start], F32, name="bank%d_%d" % (t, start), tag=tag)
             return banks[t, start][:, s0 - start : s1 - start]
 
-        def first_product(z, t, groups):
+        def first_product(z, t, spans):
             codes, scales = w1_mx[z, t]
-            ends = [s1 for s0, s1 in groups]
-            if z == PASSES - 1:
-                groups = [part for a, b in groups for part in (((a, CUT), (CUT, b)) if a < CUT < b else ((a, b),))]
-            for s0, s1 in groups:
-                nc.tensor.matmul_mx(
-                    out=in_bank(t, s0, s1),
-                    lhsT=codes.bitcast(FP8X4),
-                    lhsT_scale=scales,
-                    rhs=picked_words(z, s0, s1).bitcast(FP8X4),
-                    rhs_scale=x_plane[8 * z : P, s0:s1],
-                    start=(z == 0),
-                    stop=(z == PASSES - 1 and s1 in ends),
-                )
+            last = z == PASSES - 1
+            for start, end in spans:
+                cut = last and start < WORD_CUT < end
+                for s0, s1 in ((start, WORD_CUT), (WORD_CUT, end)) if cut else ((start, end),):
+                    nc.tensor.matmul_mx(
+                        out=in_bank(t, s0, s1),
+                        lhsT=codes.bitcast(FP8X4),
+                        lhsT_scale=scales,
+                        rhs=picked_words(z, s0, s1).bitcast(FP8X4),
+                        rhs_scale=x_plane[8 * z : P, s0:s1],
+                        start=(z == 0),
+                        stop=(last and s1 == end),
+                    )
 
         h = {}
 
@@ -188,24 +178,13 @@ def tile_picked_phpair_abs_p_kernel(
             nc.scalar.copy(h[t][:, s0:s1], in_bank(t, s0, s1))
 
         pick_words(0, 0, S, "picked0")
-        idle = psum.tile([P, BANK], F32, name="idle", tag="bank7")
-        for n in range(2):
-            nc.tensor.matmul_mx(
-                out=idle[:],
-                lhsT=picked_words(0, 0, P).bitcast(FP8X4),
-                lhsT_scale=picked_scales[:, 0:P],
-                rhs=picked_words(0, 0, BANK).bitcast(FP8X4),
-                rhs_scale=picked_scales[:, 0:BANK],
-                start=True,
-                stop=True,
-            )
         interleave_own(nc.scalar.copy, 0, 0)
         quantise_w1(0, 0, 1)
         interleave_mixed(nc.scalar.copy, 0, 0)
-        pick_words(1, 0, CUT, "picked1")
+        pick_words(1, 0, WORD_CUT, "picked1")
         interleave_own(nc.scalar.copy, 1, 0)
         quantise_w1(1, 0, 1)
-        pick_words(1, CUT, S, "picked_scales")
+        pick_words(1, WORD_CUT, S, "picked_scales")
         interleave_mixed(nc.scalar.copy, 1, 0)
         for span in SPANS[0]:
             for z in range(PASSES):
@@ -221,7 +200,8 @@ def tile_picked_phpair_abs_p_kernel(
         quantise_w1(0, 1, 1)
         for t in (1, 2, 3):
             first_product(0, t, SPANS[t])
-        stage(1, 1, 1)
+
+        stage(1, 1, 1, "w1_10_codes")
         interleave_own(nc.scalar.copy, 1, 1)
         quantise_w1(1, 1, 1)
         first_product(1, 1, SPANS[1])
@@ -239,9 +219,9 @@ def tile_picked_phpair_abs_p_kernel(
         evacuate(3, BANK, S)
         evacuate(2, S - LAST_COPY, S)
 
-        diff = placed.tile([P, 4, V], F32, name="diff", offset=LATE + 1024, align_bytes=64)
+        diff = placed.tile([P, 4, V], F32, name="diff", offset=LAST_PIECE + PIECE_BYTES // 4, align_bytes=64)
         moving = keep.tile([P, V], F32, name="moving")
-        lefts = {0: keep.tile([P, V], F32, name="left0", tag="left0", align_bytes=64)}
+        left_head = keep.tile([P, V], F32, name="left0", tag="left0", align_bytes=64)
         rings = [keep.tile([P, LEFTS[0][1]], F32, name="ring%d" % n, tag="ring%d" % n, align_bytes=64) for n in range(2)]
 
         def fetch_left(dst, t, v0, v1):
@@ -250,11 +230,11 @@ def tile_picked_phpair_abs_p_kernel(
         def subtract(dst, values, t, v0, v1):
             nc.vector.tensor_tensor(dst, h[t][:].indirect(right_sb[:, v0 // LIST : v1 // LIST]), values, SUB)
 
-        rest = placed.tile([P, V - FIRST], F32, name="left_rest", offset=LATE, align_bytes=64)
-        fetch_left(lefts[0][:, 0:FIRST], 0, 0, FIRST)
-        fetch_left(rest[:], 0, FIRST, V)
-        subtract(diff[:, 0, 0:FIRST], lefts[0][:, 0:FIRST], 0, 0, FIRST)
-        subtract(diff[:, 0, FIRST:V], rest[:], 0, FIRST, V)
+        left_rest = placed.tile([P, V - LEFT_CUT], F32, name="left_rest", offset=LAST_PIECE, align_bytes=64)
+        fetch_left(left_head[:, 0:LEFT_CUT], 0, 0, LEFT_CUT)
+        fetch_left(left_rest[:], 0, LEFT_CUT, V)
+        subtract(diff[:, 0, 0:LEFT_CUT], left_head[:, 0:LEFT_CUT], 0, 0, LEFT_CUT)
+        subtract(diff[:, 0, LEFT_CUT:V], left_rest[:], 0, LEFT_CUT, V)
         nc.sync.dma_start(diff[0:LOW, 1, :], diff[LOW:P, 0, :])
 
         w2_raw = keep.tile([P, 4 * N], F32, name="w2_raw", tag="left0", align_bytes=64)
@@ -277,8 +257,8 @@ def tile_picked_phpair_abs_p_kernel(
 
         z_grouped = []
         order = (2, 3)
-        for c, (v0, v1) in enumerate(CHUNKS):
-            fetched, upto = [stretch for stretch in LEFTS if stretch[0] <= v0][-1]
+        for c, (v0, v1) in enumerate(STRETCHES):
+            fetched, upto = [piece for piece in LEFTS if piece[0] <= v0][-1]
             if v0 == fetched:
                 order = order[::-1]
                 for t, ring in zip(order, rings):
@@ -297,10 +277,10 @@ def tile_picked_phpair_abs_p_kernel(
         z_scales = keep.tile([P, V], U8, name="z_scales", align_bytes=64)
 
         for n, group in enumerate(STORES):
-            g0, g1 = CHUNKS[group[0]][0], CHUNKS[group[-1]][1]
+            g0, g1 = STRETCHES[group[0]][0], STRETCHES[group[-1]][1]
             acc = psum.tile([P, g1 - g0], F32, name="acc%d" % n, tag="bank%d" % (2 + n))
             for c in group:
-                v0, v1 = CHUNKS[c]
+                v0, v1 = STRETCHES[c]
                 codes = z_codes[:, v0:v1].bitcast(FP8X4)
                 nc.vector.quantize_mx(out=codes, scales=z_scales[:, v0:v1], in_=z_grouped[c][:])
                 nc.tensor.matmul_mx(

@@ -33,6 +33,7 @@ STRETCHES = ((0, 256), (256, 384), (384, 448), (448, 512))
 LEFTS = ((0, 384), (384, 512))
 STORES = ((0,), (1,), (2, 3))
 LAST_COPY = 64
+WARM_UPS = 2
 
 
 def tile_picked_phpair_abs_p_kernel(
@@ -178,6 +179,17 @@ def tile_picked_phpair_abs_p_kernel(
             nc.scalar.copy(h[t][:, s0:s1], in_bank(t, s0, s1))
 
         pick_words(0, 0, S, "picked0")
+        idle = psum.tile([P, BANK], F32, name="idle", tag="bank7")
+        for n in range(WARM_UPS):
+            nc.tensor.matmul_mx(
+                out=idle[:],
+                lhsT=picked_words(0, 0, P).bitcast(FP8X4),
+                lhsT_scale=picked_scales[:, 0:P],
+                rhs=picked_words(0, 0, BANK).bitcast(FP8X4),
+                rhs_scale=picked_scales[:, 0:BANK],
+                start=True,
+                stop=True,
+            )
         interleave_own(nc.scalar.copy, 0, 0)
         quantise_w1(0, 0, 1)
         interleave_mixed(nc.scalar.copy, 0, 0)

@@ -13,27 +13,21 @@ U16 = mybir.dt.uint16
 U8 = mybir.dt.uint8
 FP8X4 = mybir.dt.float8_e4m3fn_x4
 ABS = mybir.ActivationFunctionType.Abs
+COPY = mybir.ActivationFunctionType.Copy
 SUB = mybir.AluOpType.subtract
+MULT = mybir.AluOpType.mult
+ADD = mybir.AluOpType.add
 
 P = 128
-LOW = P // 2
 PASSES = K // 512
+TILES = 4
 BANK = 512
-BANKS = 8
-HALF = H // 2
-PIECE_BYTES = 4 * HALF * 4
-LAST_PIECE = 2 * PIECE_BYTES
 LIST = 16
-QUARTERS = ((0, 256), (256, 512), (512, 768), (768, 1024))
-HALVES = ((0, 512), (512, 1024))
-SPANS = (QUARTERS, QUARTERS, HALVES, HALVES)
-WORD_CUT = 768
-LEFT_CUT = 384
+PASS_BYTES = 4 * H * 4
+MID = V // 2
+PRELOAD = 768
 STRETCHES = ((0, 256), (256, 384), (384, 448), (448, 512))
-LEFTS = ((0, 384), (384, 512))
 STORES = ((0,), (1,), (2, 3))
-LAST_COPY = 64
-WARM_UPS = 2
 
 
 def tile_picked_phpair_abs_p_kernel(
@@ -49,15 +43,17 @@ def tile_picked_phpair_abs_p_kernel(
         left_sb = keep.tile([P, V // LIST], U16, name="left_sb")
         right_sb = keep.tile([P, V // LIST], U16, name="right_sb")
 
-        w1_first = keep.tile([P, 4 * HALF], F32, name="w1_first", tag="w1_first", align_bytes=64)
-        first_rows = w1[0:512, 0:HALF].rearrange("(p j) c -> p j c", j=4)
-        first_view = w1_first[:].rearrange("p (j c) -> p j c", j=4)
-        nc.sync.dma_start(first_view[:, 0:2, :], first_rows[:, 0:2, :])
+        w1_raw = [
+            keep.tile([P, 4 * H], F32, name="w1_raw0", align_bytes=64),
+            placed.tile([P, 4 * H], F32, name="w1_raw1", offset=0, align_bytes=64),
+        ]
+        w1_rows = [w1[512 * z : 512 * (z + 1), :].rearrange("(p j) c -> p (j c)", j=4) for z in range(PASSES)]
+        nc.sync.dma_start(w1_raw[0][:, 0:PRELOAD], w1_rows[0][:, 0:PRELOAD])
         nc.sync.dma_start(offs_sb[:], offs)
         nc.sync.dma_start(left_sb[:], left)
         nc.sync.dma_start(right_sb[:], right)
 
-        scale_table = placed.tile([P, T], U8, name="scale_table", offset=LAST_PIECE - T // 2, align_bytes=64)
+        scale_table = placed.tile([P, T], U8, name="scale_table", offset=PASS_BYTES - T // 2, align_bytes=64)
         x_plane = keep.tile([P, S], U8, name="x_plane", align_bytes=64)
         nc.vector.memset(scale_table[:].bitcast(I32), 0)
         nc.vector.memset(x_plane[:].bitcast(I32), 0)
@@ -65,28 +61,14 @@ def tile_picked_phpair_abs_p_kernel(
         for e in range(2):
             nc.sync.dma_start(scale_table[e:P:8, :].bitcast(I32), scale_rows[e].bitcast(I32))
 
-        word_table = [
-            keep.tile([P, T], U32, name="word_table0", align_bytes=64),
-            keep.tile([P, T], U32, name="word_table1", align_bytes=64),
-        ]
+        word_table = [keep.tile([P, T], U32, name="word_table%d" % z, align_bytes=64) for z in range(PASSES)]
         word_rows = [x_words[z].rearrange("p c r -> p (c r)").bitcast(I32) for z in range(PASSES)]
         for c0 in (0, T // 2):
             nc.sync.dma_start(word_table[0][:, c0 : c0 + T // 2].bitcast(I32), word_rows[0][:, c0 : c0 + T // 2])
-        nc.sync.dma_start(first_view[:, 2:4, :], first_rows[:, 2:4, :])
+        nc.sync.dma_start(w1_raw[0][:, PRELOAD:], w1_rows[0][:, PRELOAD:])
         nc.sync.dma_start(word_table[1][:].bitcast(I32), word_rows[1])
 
-        w1_raw = {(0, 0): w1_first}
-
-        def load_w1(z, hf, raw):
-            nc.sync.dma_start(
-                raw[:].rearrange("p (j c) -> p j c", j=4),
-                w1[512 * z : 512 * (z + 1), HALF * hf : HALF * (hf + 1)].rearrange("(p j) c -> p j c", j=4),
-            )
-            w1_raw[z, hf] = raw
-
-        load_w1(1, 0, keep.tile([P, 4 * HALF], F32, name="w1_raw10", align_bytes=64))
-
-        picked_scales = keep.tile([P, S], U8, name="picked_scales", tag="picked_scales", align_bytes=64)
+        picked_scales = keep.tile([P, S], U8, name="picked_scales", align_bytes=64)
         nc.vector.tensor_copy(picked_scales[:], scale_table[:].indirect(offs_sb[:]))
         for e in range(2):
             nc.sync.dma_start(x_plane[e:P:8, :].bitcast(I32), picked_scales[e:P:8, :].bitcast(I32))
@@ -96,201 +78,151 @@ def tile_picked_phpair_abs_p_kernel(
                     x_plane[8 * z + 2 + e : P : 32, :].bitcast(I32),
                     picked_scales[16 + 8 * z + e : P : 32, :].bitcast(I32),
                 )
-        third = LAST_PIECE - PIECE_BYTES
-        load_w1(0, 1, placed.tile([P, 4 * HALF], F32, name="w1_raw01", offset=third, align_bytes=64))
-        load_w1(1, 1, placed.tile([P, 4 * HALF], F32, name="w1_raw11", offset=LAST_PIECE, align_bytes=64))
-
-        picked = {}
-
-        def pick_words(z, s0, s1, tag):
-            words = keep.tile([P, s1 - s0], U32, name="picked%d_%d" % (z, s0), tag=tag, align_bytes=64)
-            nc.vector.tensor_copy(words[:], word_table[z][:].indirect(offs_sb[:, s0 // LIST : s1 // LIST]))
-            picked[z, s0] = words
-
-        def picked_words(z, s0, s1):
-            start = max(a for y, a in picked if y == z and a <= s0)
-            return picked[z, start][:, s0 - start : s1 - start]
-
-        grouped = {}
-
-        def stage(z, t, tiles, tag):
-            grouped[z, t] = keep.tile([P, 4 * P * tiles], BF16, name="grouped%d%d" % (z, t), tag=tag, align_bytes=64)
-
-        stage(0, 0, 1, "grouped00")
-        stage(1, 0, 1, "grouped10")
-        stage(0, 1, 1, "grouped01")
-        stage(0, 2, 2, "left0")
-        stage(1, 2, 2, "grouped12")
-
-        def plane_pair(z, hf, pair):
-            return w1_raw[z, hf][:].rearrange("p (j g s t e) -> p s t g j e", j=4, s=2, t=2, e=4)[:, pair]
-
-        def interleave_own(copy, z, hf):
-            copy(grouped[z, hf][:].rearrange("p (t g e j) -> p t g j e", t=2, e=4, j=4), plane_pair(z, hf, 0))
-
-        def interleave_mixed(copy, z, hf):
-            copy(
-                grouped[z, 2][:].rearrange("p (t h g e j) -> p h t g j e", t=2, h=2, e=4, j=4)[:, hf],
-                plane_pair(z, hf, 1),
-            )
-
-        def quantise(values, width, name):
-            codes = keep.tile([P, width], U32, name=name + "_codes", tag=name + "_codes", align_bytes=64)
-            scales = keep.tile([P, width], U8, name=name + "_scales", tag=name + "_scales", align_bytes=64)
-            nc.vector.quantize_mx(out=codes[:].bitcast(FP8X4), scales=scales[:], in_=values[:])
-            return codes, scales
-
-        w1_mx = {}
-
-        def quantise_w1(z, t, tiles):
-            codes, scales = quantise(grouped[z, t], P * tiles, "w1_%d%d" % (z, t))
-            for n in range(tiles):
-                w1_mx[z, t + n] = (codes[:, P * n : P * (n + 1)], scales[:, P * n : P * (n + 1)])
-
-        banks = {}
-
-        def in_bank(t, s0, s1):
-            n = max(n for n, (a, b) in enumerate(SPANS[t]) if a <= s0)
-            start, end = SPANS[t][n]
-            if (t, start) not in banks:
-                tag = "bank%d" % ((sum(len(spans) for spans in SPANS[:t]) + n) % BANKS)
-                banks[t, start] = psum.tile([P, end - start], F32, name="bank%d_%d" % (t, start), tag=tag)
-            return banks[t, start][:, s0 - start : s1 - start]
-
-        def first_product(z, t, spans):
-            codes, scales = w1_mx[z, t]
-            last = z == PASSES - 1
-            for start, end in spans:
-                cut = last and start < WORD_CUT < end
-                for s0, s1 in ((start, WORD_CUT), (WORD_CUT, end)) if cut else ((start, end),):
-                    nc.tensor.matmul_mx(
-                        out=in_bank(t, s0, s1),
-                        lhsT=codes.bitcast(FP8X4),
-                        lhsT_scale=scales,
-                        rhs=picked_words(z, s0, s1).bitcast(FP8X4),
-                        rhs_scale=x_plane[8 * z : P, s0:s1],
-                        start=(z == 0),
-                        stop=(last and s1 == end),
-                    )
-
-        h = {}
-
-        def evacuate(t, s0, s1):
-            nc.scalar.copy(h[t][:, s0:s1], in_bank(t, s0, s1))
-
-        pick_words(0, 0, S, "picked0")
-        idle = psum.tile([P, BANK], F32, name="idle", tag="bank7")
-        for n in range(WARM_UPS):
-            nc.tensor.matmul_mx(
-                out=idle[:],
-                lhsT=picked_words(0, 0, P).bitcast(FP8X4),
-                lhsT_scale=picked_scales[:, 0:P],
-                rhs=picked_words(0, 0, BANK).bitcast(FP8X4),
-                rhs_scale=picked_scales[:, 0:BANK],
-                start=True,
-                stop=True,
-            )
-        interleave_own(nc.scalar.copy, 0, 0)
-        quantise_w1(0, 0, 1)
-        interleave_mixed(nc.scalar.copy, 0, 0)
-        pick_words(1, 0, WORD_CUT, "picked1")
-        interleave_own(nc.scalar.copy, 1, 0)
-        quantise_w1(1, 0, 1)
-        pick_words(1, WORD_CUT, S, "picked_scales")
-        interleave_mixed(nc.scalar.copy, 1, 0)
-        for span in SPANS[0]:
-            for z in range(PASSES):
-                first_product(z, 0, [span])
-        for t in range(4):
-            h[t] = keep.tile([P, S], F32, name="h%d" % t)
-        for s0, s1 in SPANS[0]:
-            evacuate(0, s0, s1)
-
-        interleave_mixed(nc.vector.tensor_copy, 0, 1)
-        interleave_own(nc.vector.tensor_copy, 0, 1)
-        quantise_w1(0, 2, 2)
-        quantise_w1(0, 1, 1)
-        for t in (1, 2, 3):
-            first_product(0, t, SPANS[t])
-
-        stage(1, 1, 1, "w1_10_codes")
-        interleave_own(nc.scalar.copy, 1, 1)
-        quantise_w1(1, 1, 1)
-        first_product(1, 1, SPANS[1])
-        interleave_mixed(nc.scalar.copy, 1, 1)
-        quantise_w1(1, 2, 2)
-
-        for s0, s1 in SPANS[1]:
-            evacuate(1, s0, s1)
-        for bank in range(2):
-            for t in (2, 3):
-                first_product(1, t, SPANS[t][bank : bank + 1])
-        evacuate(2, 0, BANK)
-        evacuate(3, 0, BANK)
-        evacuate(2, BANK, S - LAST_COPY)
-        evacuate(3, BANK, S)
-        evacuate(2, S - LAST_COPY, S)
-
-        diff = placed.tile([P, 4, V], F32, name="diff", offset=LAST_PIECE + PIECE_BYTES // 4, align_bytes=64)
-        moving = keep.tile([P, V], F32, name="moving")
-        left_head = keep.tile([P, V], F32, name="left0", tag="left0", align_bytes=64)
-        rings = [keep.tile([P, LEFTS[0][1]], F32, name="ring%d" % n, tag="ring%d" % n, align_bytes=64) for n in range(2)]
-
-        def fetch_left(dst, t, v0, v1):
-            nc.vector.tensor_copy(dst, h[t][:].indirect(left_sb[:, v0 // LIST : v1 // LIST]))
-
-        def subtract(dst, values, t, v0, v1):
-            nc.vector.tensor_tensor(dst, h[t][:].indirect(right_sb[:, v0 // LIST : v1 // LIST]), values, SUB)
-
-        left_rest = placed.tile([P, V - LEFT_CUT], F32, name="left_rest", offset=LAST_PIECE, align_bytes=64)
-        fetch_left(left_head[:, 0:LEFT_CUT], 0, 0, LEFT_CUT)
-        fetch_left(left_rest[:], 0, LEFT_CUT, V)
-        subtract(diff[:, 0, 0:LEFT_CUT], left_head[:, 0:LEFT_CUT], 0, 0, LEFT_CUT)
-        subtract(diff[:, 0, LEFT_CUT:V], left_rest[:], 0, LEFT_CUT, V)
-        nc.sync.dma_start(diff[0:LOW, 1, :], diff[LOW:P, 0, :])
-
-        w2_raw = keep.tile([P, 4 * N], F32, name="w2_raw", tag="left0", align_bytes=64)
+        nc.sync.dma_start(w1_raw[1][:], w1_rows[1])
+        w2_raw = placed.tile([P, 4 * N], F32, name="w2_raw", offset=PASS_BYTES, align_bytes=64)
         w2_rows = w2.rearrange("(g t e) m -> t g e m", t=4, e=4)
         for t in range(4):
             nc.sync.dma_start(w2_raw[:, t * N : (t + 1) * N], w2_rows[t])
-        w2_grouped = keep.tile([P, 4 * N], BF16, name="w2_grouped", align_bytes=64)
-        nc.scalar.copy(
+
+        picked = {}
+
+        def pick_words(z, tag):
+            picked[z] = keep.tile([P, S], U32, name="picked%d" % z, tag=tag, align_bytes=64)
+            nc.vector.tensor_copy(picked[z][:], word_table[z][:].indirect(offs_sb[:]))
+
+        groups = (((0, 0),), ((0, 1),), ((0, 2),), ((1, 0),), ((1, 1),), ((0, 3), (1, 2), (1, 3)))
+        staged = {}
+        for group in groups:
+            tile = keep.tile([P, len(group) * 4 * P], BF16, name="grouped%d%d" % group[0], tag="grouped%d%d" % group[0], align_bytes=64)
+            for n, operand in enumerate(group):
+                staged[operand] = (tile, n)
+        w1_mx = {}
+
+        def interleave(copy, z, t):
+            tile, n = staged[z, t]
+            copy(
+                tile[:, 4 * P * n : 4 * P * (n + 1)].rearrange("p (g e j) -> p g j e", e=4, j=4),
+                w1_raw[z][:].rearrange("p (j g t e) -> p t g j e", j=4, t=4, e=4)[:, t],
+            )
+
+        def quantise(values, width, name, scales):
+            codes = keep.tile([P, width], U32, name=name + "_codes", align_bytes=64)
+            nc.vector.quantize_mx(out=codes[:].bitcast(FP8X4), scales=scales, in_=values)
+            return codes
+
+        shared_scales = keep.tile([P, P], U8, name="shared_scales", align_bytes=64)
+        planes = {(0, 2): shared_scales[4:P, :], (1, 0): shared_scales[:]}
+
+        def quantise_w1(group):
+            name, width = "w1_%d%d" % group[0], P * len(group)
+            if group[0] not in planes:
+                planes[group[0]] = keep.tile([P, width], U8, name=name + "_scales", align_bytes=64)[:]
+            scales = planes[group[0]]
+            codes = quantise(staged[group[0]][0][:], width, name, scales)
+            for n, operand in enumerate(group):
+                w1_mx[operand] = (codes[:, P * n : P * (n + 1)], scales[:, P * n : P * (n + 1)])
+
+        banks = {
+            (t, b): psum.tile([P, BANK], F32, name="bank%d_%d" % (t, b), tag="bank%d" % (2 * t + b))
+            for t in range(TILES)
+            for b in range(2)
+        }
+
+        def first_product(z, t, b):
+            codes, scales = w1_mx[z, t]
+            cols = slice(BANK * b, BANK * (b + 1))
+            nc.tensor.matmul_mx(
+                out=banks[t, b][:],
+                lhsT=codes.bitcast(FP8X4),
+                lhsT_scale=scales,
+                rhs=picked[z][:, cols].bitcast(FP8X4),
+                rhs_scale=x_plane[8 * z : P, cols],
+                start=(z == 0),
+                stop=(z == PASSES - 1),
+            )
+
+        pick_words(0, "picked0")
+        interleave(nc.scalar.copy, 0, 0)
+        interleave(nc.scalar.copy, 0, 1)
+        interleave(nc.scalar.copy, 0, 2)
+        interleave(nc.scalar.copy, 0, 3)
+        for n in (0, 1, 2):
+            quantise_w1(groups[n])
+        pick_words(1, "grouped02")
+
+        interleave(nc.vector.tensor_copy, 1, 0)
+        interleave(nc.vector.tensor_copy, 1, 1)
+        interleave(nc.scalar.copy, 1, 2)
+        interleave(nc.scalar.copy, 1, 3)
+        for group in groups[3:]:
+            quantise_w1(group)
+        for z, t in ((0, 0), (0, 1), (1, 0), (1, 1), (0, 2), (1, 2)):
+            for b in range(2):
+                first_product(z, t, b)
+        for b in range(2):
+            for z in range(PASSES):
+                first_product(z, 3, b)
+
+        w2_grouped = keep.tile([P, 4 * N], BF16, name="w2_grouped", tag="grouped03", align_bytes=64)
+        nc.gpsimd.tensor_scalar(
             w2_grouped[:].rearrange("p (c n t) -> p c t n", n=4, t=4),
             w2_raw[:].rearrange("p (t c n) -> p c t n", t=4, n=4),
+            1.0,
+            0.0,
+            MULT,
+            ADD,
         )
+        h = [keep.tile([P, S], F32, name="h%d" % t) for t in range(TILES)]
+        lefts = [keep.tile([P, V], F32, name="lefts%d" % t, tag="lefts%d" % t, align_bytes=64) for t in range(TILES)]
+        diff = keep.tile([P, TILES, V], F32, name="diff", align_bytes=64)
 
-        halves = ((0, V // 2), (V // 2, V))
-        for (v0, v1), ring in zip(halves, rings):
-            fetch_left(ring[:, 0 : v1 - v0], 1, v0, v1)
-        for (v0, v1), ring in zip(halves, rings):
-            subtract(moving[:, v0:v1], ring[:, 0 : v1 - v0], 1, v0, v1)
-            nc.sync.dma_start(diff[LOW:P, 0, v0:v1], moving[0:LOW, v0:v1])
-            nc.sync.dma_start(diff[LOW:P, 1, v0:v1], moving[LOW:P, v0:v1])
+        def evacuate(copy, t, s0, s1):
+            b = s0 // BANK
+            copy(h[t][:, s0:s1], banks[t, b][:, s0 - BANK * b : s1 - BANK * b])
 
-        z_grouped = []
-        order = (2, 3)
+        def fetch_left(t, v0, v1):
+            nc.scalar.activation(lefts[t][:, v0:v1], h[t][:].indirect(left_sb[:, v0 // LIST : v1 // LIST]), COPY)
+
+        def subtract(t, v0, v1):
+            nc.vector.tensor_tensor(
+                diff[:, t, v0:v1], h[t][:].indirect(right_sb[:, v0 // LIST : v1 // LIST]), lefts[t][:, v0:v1], SUB
+            )
+
+        evacuate(nc.scalar.copy, 0, 0, BANK)
+        evacuate(nc.vector.tensor_copy, 0, BANK, S)
+        evacuate(nc.scalar.copy, 1, 0, BANK)
+        evacuate(nc.vector.tensor_copy, 1, BANK, S)
+        fetch_left(0, 0, V)
+        fetch_left(1, 0, V)
+        evacuate(nc.vector.tensor_copy, 2, 0, BANK)
+        evacuate(nc.vector.tensor_copy, 2, BANK, S)
+        evacuate(nc.vector.tensor_copy, 3, 0, BANK)
+        subtract(0, 0, V)
+        evacuate(nc.scalar.copy, 3, BANK, S)
+        subtract(1, 0, V)
+        for v0, v1 in ((0, MID), (MID, V)):
+            for t in (2, 3):
+                fetch_left(t, v0, v1)
+
+        z_grouped = {}
         for c, (v0, v1) in enumerate(STRETCHES):
-            fetched, upto = [piece for piece in LEFTS if piece[0] <= v0][-1]
-            if v0 == fetched:
-                order = order[::-1]
-                for t, ring in zip(order, rings):
-                    fetch_left(ring[:, 0 : upto - v0], t, v0, upto)
-            for t, ring in zip(order, rings):
-                subtract(diff[:, t, v0:v1], ring[:, v0 - fetched : v1 - fetched], t, v0, v1)
-            z_grouped.append(keep.tile([P, 4 * (v1 - v0)], BF16, name="z_grouped%d" % c, align_bytes=64))
+            for t in (2, 3):
+                subtract(t, v0, v1)
+            if c == 2:
+                w2_scales = keep.tile([P, N], U8, name="w2_scales", tag="lefts1", align_bytes=64)
+                w2_codes = quantise(w2_grouped[:], N, "w2", w2_scales[:])
+            z_grouped[c] = keep.tile([P, 4 * (v1 - v0)], BF16, name="z_grouped%d" % c, align_bytes=64)
             nc.scalar.activation(
                 z_grouped[c][:].rearrange("p (c n t) -> p c t n", n=4, t=4),
                 diff[:, :, v0:v1].rearrange("p t (c n) -> p c t n", n=4),
                 ABS,
             )
 
-        w2_codes, w2_scales = quantise(w2_grouped, N, "w2")
-        z_codes = keep.tile([P, V], U32, name="z_codes", tag="ring0", align_bytes=64)
+        z_codes = keep.tile([P, V], U32, name="z_codes", align_bytes=64)
         z_scales = keep.tile([P, V], U8, name="z_scales", align_bytes=64)
-
         for n, group in enumerate(STORES):
             g0, g1 = STRETCHES[group[0]][0], STRETCHES[group[-1]][1]
-            acc = psum.tile([P, g1 - g0], F32, name="acc%d" % n, tag="bank%d" % (2 + n))
+            acc = psum.tile([P, g1 - g0], F32, name="acc%d" % n, tag="bank%d" % n)
             for c in group:
                 v0, v1 = STRETCHES[c]
                 codes = z_codes[:, v0:v1].bitcast(FP8X4)

@@ -25,6 +25,8 @@ BANK = 512
 LIST = 16
 PASS_BYTES = 4 * H * 4
 MID = V // 2
+SPANS = (((0, 256), (256, 512), (512, 1024)),) + (((0, 512), (512, 1024)),) * 3
+BANK_OF = ((0, 1, 2), (3, 4), (5, 6), (7, 0))
 PRELOAD = 768
 STRETCHES = ((0, 256), (256, 384), (384, 448), (448, 512))
 STORES = ((0,), (1,), (2, 3))
@@ -122,15 +124,14 @@ def tile_picked_phpair_abs_p_kernel(
             for n, operand in enumerate(group):
                 w1_mx[operand] = (codes[:, P * n : P * (n + 1)], scales[:, P * n : P * (n + 1)])
 
-        banks = {
-            (t, b): psum.tile([P, BANK], F32, name="bank%d_%d" % (t, b), tag="bank%d" % (2 * t + b))
-            for t in range(TILES)
-            for b in range(2)
-        }
+        banks = {}
 
         def first_product(z, t, b):
             codes, scales = w1_mx[z, t]
-            cols = slice(BANK * b, BANK * (b + 1))
+            start, end = SPANS[t][b]
+            cols = slice(start, end)
+            if z == 0:
+                banks[t, b] = psum.tile([P, end - start], F32, name="bank%d_%d" % (t, b), tag="bank%d" % BANK_OF[t][b])
             nc.tensor.matmul_mx(
                 out=banks[t, b][:],
                 lhsT=codes.bitcast(FP8X4),
@@ -157,7 +158,7 @@ def tile_picked_phpair_abs_p_kernel(
         for group in groups[3:]:
             quantise_w1(group)
         for z, t in ((0, 0), (0, 1), (1, 0), (1, 1), (0, 2), (1, 2)):
-            for b in range(2):
+            for b in range(len(SPANS[t])):
                 first_product(z, t, b)
         for b in range(2):
             for z in range(PASSES):
@@ -176,9 +177,9 @@ def tile_picked_phpair_abs_p_kernel(
         lefts = [keep.tile([P, V], F32, name="lefts%d" % t, tag="lefts%d" % t, align_bytes=64) for t in range(TILES)]
         diff = keep.tile([P, TILES, V], F32, name="diff", align_bytes=64)
 
-        def evacuate(copy, t, s0, s1):
-            b = s0 // BANK
-            copy(h[t][:, s0:s1], banks[t, b][:, s0 - BANK * b : s1 - BANK * b])
+        def evacuate(copy, t, b):
+            start, end = SPANS[t][b]
+            copy(h[t][:, start:end], banks[t, b][:])
 
         def fetch_left(t, v0, v1):
             nc.scalar.activation(lefts[t][:, v0:v1], h[t][:].indirect(left_sb[:, v0 // LIST : v1 // LIST]), COPY)
@@ -188,17 +189,18 @@ def tile_picked_phpair_abs_p_kernel(
                 diff[:, t, v0:v1], h[t][:].indirect(right_sb[:, v0 // LIST : v1 // LIST]), lefts[t][:, v0:v1], SUB
             )
 
-        evacuate(nc.scalar.copy, 0, 0, BANK)
-        evacuate(nc.vector.tensor_copy, 0, BANK, S)
-        evacuate(nc.scalar.copy, 1, 0, BANK)
-        evacuate(nc.vector.tensor_copy, 1, BANK, S)
+        evacuate(nc.scalar.copy, 0, 0)
+        evacuate(nc.vector.tensor_copy, 0, 1)
+        evacuate(nc.scalar.copy, 0, 2)
+        evacuate(nc.scalar.copy, 1, 0)
+        evacuate(nc.vector.tensor_copy, 1, 1)
         fetch_left(0, 0, V)
         fetch_left(1, 0, V)
-        evacuate(nc.vector.tensor_copy, 2, 0, BANK)
-        evacuate(nc.vector.tensor_copy, 2, BANK, S)
-        evacuate(nc.vector.tensor_copy, 3, 0, BANK)
+        evacuate(nc.vector.tensor_copy, 2, 0)
+        evacuate(nc.vector.tensor_copy, 2, 1)
+        evacuate(nc.vector.tensor_copy, 3, 0)
         subtract(0, 0, V)
-        evacuate(nc.scalar.copy, 3, BANK, S)
+        evacuate(nc.scalar.copy, 3, 1)
         subtract(1, 0, V)
         for v0, v1 in ((0, MID), (MID, V)):
             for t in (2, 3):
@@ -222,7 +224,7 @@ def tile_picked_phpair_abs_p_kernel(
         z_scales = keep.tile([P, V], U8, name="z_scales", align_bytes=64)
         for n, group in enumerate(STORES):
             g0, g1 = STRETCHES[group[0]][0], STRETCHES[group[-1]][1]
-            acc = psum.tile([P, g1 - g0], F32, name="acc%d" % n, tag="bank%d" % n)
+            acc = psum.tile([P, g1 - g0], F32, name="acc%d" % n, tag="bank%d" % (1 + n))
             for c in group:
                 v0, v1 = STRETCHES[c]
                 codes = z_codes[:, v0:v1].bitcast(FP8X4)

@@ -25,7 +25,7 @@ BANK = 512
 LIST = 16
 PASS_BYTES = 4 * H * 4
 MID = V // 2
-SPANS = (((0, 256), (256, 512), (512, 1024)),) + (((0, 512), (512, 1024)),) * 3
+SPANS = (((0, 256), (256, 768), (768, 1024)),) + (((0, 512), (512, 1024)),) * 3
 BANK_OF = ((0, 1, 2), (3, 4), (5, 6), (7, 0))
 PRELOAD = 768
 STRETCHES = ((0, 256), (256, 384), (384, 448), (448, 512))
@@ -112,14 +112,9 @@ def tile_picked_phpair_abs_p_kernel(
             nc.vector.quantize_mx(out=codes[:].bitcast(FP8X4), scales=scales, in_=values)
             return codes
 
-        shared_scales = keep.tile([P, P], U8, name="shared_scales", align_bytes=64)
-        planes = {(0, 2): shared_scales[4:P, :], (1, 0): shared_scales[:]}
-
         def quantise_w1(group):
             name, width = "w1_%d%d" % group[0], P * len(group)
-            if group[0] not in planes:
-                planes[group[0]] = keep.tile([P, width], U8, name=name + "_scales", align_bytes=64)[:]
-            scales = planes[group[0]]
+            scales = keep.tile([P, width], U8, name=name + "_scales", align_bytes=64)[:]
             codes = quantise(staged[group[0]][0][:], width, name, scales)
             for n, operand in enumerate(group):
                 w1_mx[operand] = (codes[:, P * n : P * (n + 1)], scales[:, P * n : P * (n + 1)])
@@ -157,7 +152,7 @@ def tile_picked_phpair_abs_p_kernel(
         interleave(nc.scalar.copy, 1, 3)
         for group in groups[3:]:
             quantise_w1(group)
-        for z, t in ((0, 0), (0, 1), (1, 0), (1, 1), (0, 2), (1, 2)):
+        for z, t in ((0, 0), (0, 1), (0, 2), (1, 0), (1, 1), (1, 2)):
             for b in range(len(SPANS[t])):
                 first_product(z, t, b)
         for b in range(2):
@@ -190,10 +185,10 @@ def tile_picked_phpair_abs_p_kernel(
             )
 
         evacuate(nc.scalar.copy, 0, 0)
-        evacuate(nc.vector.tensor_copy, 0, 1)
-        evacuate(nc.scalar.copy, 0, 2)
-        evacuate(nc.scalar.copy, 1, 0)
-        evacuate(nc.vector.tensor_copy, 1, 1)
+        evacuate(nc.scalar.copy, 0, 1)
+        evacuate(nc.vector.tensor_copy, 0, 2)
+        evacuate(nc.vector.tensor_copy, 1, 0)
+        evacuate(nc.scalar.copy, 1, 1)
         fetch_left(0, 0, V)
         fetch_left(1, 0, V)
         evacuate(nc.vector.tensor_copy, 2, 0)

from contextlib import ExitStack

import concourse.mybir as mybir

K, T, S, H, N, V = 1024, 2048, 1024, 512, 128, 512
FLOPS = 2 * K * H * S + 2 * H * N * V

F32 = mybir.dt.float32
BF16 = mybir.dt.bfloat16
I32 = mybir.dt.int32
U32 = mybir.dt.uint32
U16 = mybir.dt.uint16
U8 = mybir.dt.uint8
FP8X4 = mybir.dt.float8_e4m3fn_x4
ABS = mybir.ActivationFunctionType.Abs
COPY = mybir.ActivationFunctionType.Copy
SUB = mybir.AluOpType.subtract
MULT = mybir.AluOpType.mult
ADD = mybir.AluOpType.add

P = 128
PASSES = K // 512
TILES = 4
BANK = 512
LIST = 16
PASS_BYTES = 4 * H * 4
MID = V // 2
SPANS = (((0, 256), (256, 768), (768, 1024)),) + (((0, 512), (512, 1024)),) * 3
BANK_OF = ((0, 1, 2), (3, 4), (5, 6), (7, 0))
PRELOAD = 768
STRETCHES = ((0, 256), (256, 384), (384, 448), (448, 512))
STORES = ((0,), (1,), (2, 3))


def tile_picked_phpair_abs_p_kernel(
    tc, x_words, x_scales, w1, w2, offs, left, right, out
):
    nc = tc.nc
    with ExitStack() as ctx:
        keep = ctx.enter_context(tc.tile_pool(name="keep", bufs=1))
        placed = ctx.enter_context(tc.tile_pool(name="placed", bufs=1))
        psum = ctx.enter_context(tc.psum_pool(name="psum", bufs=1))

        offs_sb = keep.tile([P, S // LIST], U16, name="offs_sb")
        left_sb = keep.tile([P, V // LIST], U16, name="left_sb")
        right_sb = keep.tile([P, V // LIST], U16, name="right_sb")

        w1_raw = [
            keep.tile([P, 4 * H], F32, name="w1_raw0", align_bytes=64),
            placed.tile([P, 4 * H], F32, name="w1_raw1", offset=0, align_bytes=64),
        ]
        w1_rows = [w1[512 * z : 512 * (z + 1), :].rearrange("(p j) c -> p (j c)", j=4) for z in range(PASSES)]
        nc.sync.dma_start(w1_raw[0][:, 0:PRELOAD], w1_rows[0][:, 0:PRELOAD])
        nc.sync.dma_start(offs_sb[:], offs)
        nc.sync.dma_start(left_sb[:], left)
        nc.sync.dma_start(right_sb[:], right)

        scale_table = placed.tile([P, T], U8, name="scale_table", offset=PASS_BYTES - T // 2, align_bytes=64)
        x_plane = keep.tile([P, S], U8, name="x_plane", align_bytes=64)
        nc.vector.memset(scale_table[:].bitcast(I32), 0)
        nc.vector.memset(x_plane[:].bitcast(I32), 0)
        scale_rows = x_scales.rearrange("z (r e) c -> e r z c", e=2)
        for e in range(2):
            nc.sync.dma_start(scale_table[e:P:8, :].bitcast(I32), scale_rows[e].bitcast(I32))

        word_table = [keep.tile([P, T], U32, name="word_table%d" % z, align_bytes=64) for z in range(PASSES)]
        word_rows = [x_words[z].rearrange("p c r -> p (c r)").bitcast(I32) for z in range(PASSES)]
        for c0 in (0, T // 2):
            nc.sync.dma_start(word_table[0][:, c0 : c0 + T // 2].bitcast(I32), word_rows[0][:, c0 : c0 + T // 2])
        nc.sync.dma_start(w1_raw[0][:, PRELOAD:], w1_rows[0][:, PRELOAD:])
        nc.sync.dma_start(word_table[1][:].bitcast(I32), word_rows[1])

        picked_scales = keep.tile([P, S], U8, name="picked_scales", align_bytes=64)
        nc.vector.tensor_copy(picked_scales[:], scale_table[:].indirect(offs_sb[:]))
        for e in range(2):
            nc.sync.dma_start(x_plane[e:P:8, :].bitcast(I32), picked_scales[e:P:8, :].bitcast(I32))
        for z in range(PASSES):
            for e in range(2):
                nc.sync.dma_start(
                    x_plane[8 * z + 2 + e : P : 32, :].bitcast(I32),
                    picked_scales[16 + 8 * z + e : P : 32, :].bitcast(I32),
                )
        nc.sync.dma_start(w1_raw[1][:], w1_rows[1])
        w2_raw = placed.tile([P, 4 * N], F32, name="w2_raw", offset=PASS_BYTES, align_bytes=64)
        w2_rows = w2.rearrange("(g t e) m -> t g e m", t=4, e=4)
        for t in range(4):
            nc.sync.dma_start(w2_raw[:, t * N : (t + 1) * N], w2_rows[t])

        picked = {}

        def pick_words(z, tag):
            picked[z] = keep.tile([P, S], U32, name="picked%d" % z, tag=tag, align_bytes=64)
            nc.vector.tensor_copy(picked[z][:], word_table[z][:].indirect(offs_sb[:]))

        groups = (((0, 0),), ((0, 1),), ((0, 2),), ((1, 0),), ((1, 1),), ((0, 3), (1, 2), (1, 3)))
        staged = {}
        for group in groups:
            tile = keep.tile([P, len(group) * 4 * P], BF16, name="grouped%d%d" % group[0], tag="grouped%d%d" % group[0], align_bytes=64)
            for n, operand in enumerate(group):
                staged[operand] = (tile, n)
        w1_mx = {}

        def interleave(copy, z, t):
            tile, n = staged[z, t]
            copy(
                tile[:, 4 * P * n : 4 * P * (n + 1)].rearrange("p (g e j) -> p g j e", e=4, j=4),
                w1_raw[z][:].rearrange("p (j g t e) -> p t g j e", j=4, t=4, e=4)[:, t],
            )

        def quantise(values, width, name, scales):
            codes = keep.tile([P, width], U32, name=name + "_codes", align_bytes=64)
            nc.vector.quantize_mx(out=codes[:].bitcast(FP8X4), scales=scales, in_=values)
            return codes

        def quantise_w1(group):
            name, width = "w1_%d%d" % group[0], P * len(group)
            scales = keep.tile([P, width], U8, name=name + "_scales", align_bytes=64)[:]
            codes = quantise(staged[group[0]][0][:], width, name, scales)
            for n, operand in enumerate(group):
                w1_mx[operand] = (codes[:, P * n : P * (n + 1)], scales[:, P * n : P * (n + 1)])

        banks = {}

        def first_product(z, t, b):
            codes, scales = w1_mx[z, t]
            start, end = SPANS[t][b]
            cols = slice(start, end)
            if z == 0:
                banks[t, b] = psum.tile([P, end - start], F32, name="bank%d_%d" % (t, b), tag="bank%d" % BANK_OF[t][b])
            nc.tensor.matmul_mx(
                out=banks[t, b][:],
                lhsT=codes.bitcast(FP8X4),
                lhsT_scale=scales,
                rhs=picked[z][:, cols].bitcast(FP8X4),
                rhs_scale=x_plane[8 * z : P, cols],
                start=(z == 0),
                stop=(z == PASSES - 1),
            )

        pick_words(0, "picked0")
        interleave(nc.scalar.copy, 0, 0)
        interleave(nc.scalar.copy, 0, 1)
        interleave(nc.scalar.copy, 0, 2)
        interleave(nc.scalar.copy, 0, 3)
        for n in (0, 1, 2):
            quantise_w1(groups[n])
        pick_words(1, "grouped02")

        interleave(nc.vector.tensor_copy, 1, 0)
        interleave(nc.vector.tensor_copy, 1, 1)
        interleave(nc.scalar.copy, 1, 2)
        interleave(nc.scalar.copy, 1, 3)
        for group in groups[3:]:
            quantise_w1(group)
        for z, t in ((0, 0), (0, 1), (0, 2), (1, 0), (1, 1), (1, 2)):
            for b in range(len(SPANS[t])):
                first_product(z, t, b)
        for b in range(2):
            for z in range(PASSES):
                first_product(z, 3, b)

        w2_grouped = keep.tile([P, 4 * N], BF16, name="w2_grouped", tag="grouped03", align_bytes=64)
        nc.gpsimd.tensor_scalar(
            w2_grouped[:].rearrange("p (c n t) -> p c t n", n=4, t=4),
            w2_raw[:].rearrange("p (t c n) -> p c t n", t=4, n=4),
            1.0,
            0.0,
            MULT,
            ADD,
        )
        h = [keep.tile([P, S], F32, name="h%d" % t) for t in range(TILES)]
        lefts = [keep.tile([P, V], F32, name="lefts%d" % t, tag="lefts%d" % t, align_bytes=64) for t in range(TILES)]
        diff = keep.tile([P, TILES, V], F32, name="diff", align_bytes=64)

        def evacuate(copy, t, b):
            start, end = SPANS[t][b]
            copy(h[t][:, start:end], banks[t, b][:])

        def fetch_left(t, v0, v1):
            nc.scalar.activation(lefts[t][:, v0:v1], h[t][:].indirect(left_sb[:, v0 // LIST : v1 // LIST]), COPY)

        def subtract(t, v0, v1):
            nc.vector.tensor_tensor(
                diff[:, t, v0:v1], h[t][:].indirect(right_sb[:, v0 // LIST : v1 // LIST]), lefts[t][:, v0:v1], SUB
            )

        evacuate(nc.scalar.copy, 0, 0)
        evacuate(nc.scalar.copy, 0, 1)
        evacuate(nc.vector.tensor_copy, 0, 2)
        evacuate(nc.vector.tensor_copy, 1, 0)
        evacuate(nc.scalar.copy, 1, 1)
        fetch_left(0, 0, V)
        fetch_left(1, 0, V)
        evacuate(nc.vector.tensor_copy, 2, 0)
        evacuate(nc.vector.tensor_copy, 2, 1)
        evacuate(nc.vector.tensor_copy, 3, 0)
        subtract(0, 0, V)
        evacuate(nc.scalar.copy, 3, 1)
        subtract(1, 0, V)
        for v0, v1 in ((0, MID), (MID, V)):
            for t in (2, 3):
                fetch_left(t, v0, v1)

        z_grouped = {}
        for c, (v0, v1) in enumerate(STRETCHES):
            for t in (2, 3):
                subtract(t, v0, v1)
            if c == 2:
                w2_scales = keep.tile([P, N], U8, name="w2_scales", tag="lefts1", align_bytes=64)
                w2_codes = quantise(w2_grouped[:], N, "w2", w2_scales[:])
            z_grouped[c] = keep.tile([P, 4 * (v1 - v0)], BF16, name="z_grouped%d" % c, align_bytes=64)
            nc.scalar.activation(
                z_grouped[c][:].rearrange("p (c n t) -> p c t n", n=4, t=4),
                diff[:, :, v0:v1].rearrange("p t (c n) -> p c t n", n=4),
                ABS,
            )

        z_codes = keep.tile([P, V], U32, name="z_codes", align_bytes=64)
        z_scales = keep.tile([P, V], U8, name="z_scales", align_bytes=64)
        for n, group in enumerate(STORES):
            g0, g1 = STRETCHES[group[0]][0], STRETCHES[group[-1]][1]
            acc = psum.tile([P, g1 - g0], F32, name="acc%d" % n, tag="bank%d" % (1 + n))
            for c in group:
                v0, v1 = STRETCHES[c]
                codes = z_codes[:, v0:v1].bitcast(FP8X4)
                nc.vector.quantize_mx(out=codes, scales=z_scales[:, v0:v1], in_=z_grouped[c][:])
                nc.tensor.matmul_mx(
                    out=acc[:, v0 - g0 : v1 - g0],
                    lhsT=w2_codes[:].bitcast(FP8X4),
                    lhsT_scale=w2_scales[:],
                    rhs=codes,
                    rhs_scale=z_scales[:, v0:v1],
                    start=True,
                    stop=True,
                )
            result = keep.tile([P, g1 - g0], F32, name="result%d" % n)
            copy = nc.vector.tensor_copy if n == len(STORES) - 1 else nc.scalar.copy
            copy(result[:], acc[:])
            nc.sync.dma_start(out[:, g0:g1], result[:])
